import numpy as np
import ml_dtypes


def mxq(x, axis, fmt="e4m3"):
    dtype, down = {"e4m3": (ml_dtypes.float8_e4m3fn, 7), "e5m2": (ml_dtypes.float8_e5m2, 14)}[fmt]
    v = np.moveaxis(np.asarray(x, np.float32).astype(ml_dtypes.bfloat16).astype(np.float64), axis, -1)
    blocks = v.reshape(v.shape[:-1] + (-1, 32))
    amax = np.abs(blocks).max(-1, keepdims=True)
    byte = np.maximum(np.where(amax > 0, np.frexp(amax)[1] - 1 + 127, 0) - down, 1)
    scale = np.exp2(byte - 127.0)
    codes = (blocks / scale).astype(np.float32).astype(dtype).astype(np.float64)
    return np.moveaxis((codes * scale).reshape(v.shape), -1, axis)


WIDE = False


def mx_kscale(k):
    if not WIDE:
        return np.ones(k)
    levels = np.array([10, -10, 5, -5, 0])
    if k % 512:
        return np.exp2(np.random.permutation(np.resize(levels, k // 32))).repeat(32)
    a = np.empty((k // 512, 16))
    for p in range(k // 512):
        a[p, :8] = np.random.permutation(np.resize(levels, 8))
        for g in range(8):
            far = levels[np.abs(levels - a[p, g]) >= 10]
            a[p, g + 8] = far[np.random.randint(len(far))]
    return np.exp2(a.ravel()).repeat(32)


BF16 = ml_dtypes.bfloat16


def bf(x):
    return np.asarray(x, np.float32).astype(BF16)


def f64(x):
    return np.asarray(x).astype(np.float64)


S, K, M = 1024, 1024, 1024


def psi(t):
    return t * np.abs(t)


def draw0():
    s, t = mx_kscale(K), mx_kscale(M)
    row = np.exp(0.2 * np.random.standard_normal((S, 1)))
    x = np.random.standard_normal((S, K)) * row / s[None, :]
    a = np.random.standard_normal((M, K)) / np.sqrt(K) * t[:, None] * s[None, :]
    w = (1.0 + 0.1 * np.random.standard_normal(M)) / t**3
    d = 0.01 * np.sqrt(K / M) * (1.0 + 0.1 * np.random.standard_normal(K)) / s
    return {"x": bf(x), "a": bf(a), "w": bf(w), "d": bf(d)}


def core(x, a, w, d):
    af = f64(a)
    y = mxq(f64(x), 1, "e4m3") @ mxq(af, 1, "e4m3").T
    u = f64(w)[None, :] * y * np.abs(y)
    t = mxq(u, 1, "e4m3") @ mxq(af, 0, "e4m3")
    z = f64(d)[None, :] * t
    az = np.abs(z)
    cube_mean = np.mean(az * az * az, axis=-1, keepdims=True)
    nrm = np.power(cube_mean + 1e-6, 2.0 / 3.0)
    return psi(z) / nrm


def e4m3fn_bytes(y):
    return np.clip(np.asarray(y, np.float64), -448.0, 448.0).astype(np.float32).astype(ml_dtypes.float8_e4m3fn).view(np.uint8)


def e4m3fn_values(b):
    return np.asarray(b, np.uint8).view(ml_dtypes.float8_e4m3fn).astype(np.float64)


def setup_inputs():
    d = draw0()
    x0 = np.asarray(d['x']).astype(np.float64)
    s = (np.max(np.abs(x0), axis=(0,), keepdims=True) / 448.0).astype(np.float32)
    out = {}
    for k, v in d.items():
        if k == 'x':
            out['x_bytes'] = e4m3fn_bytes(x0 / s.astype(np.float64))
            out['x_scale'] = s
        else:
            out[k] = v
    return out


def reference(x_bytes, x_scale, a, w, d):
    return core(e4m3fn_values(x_bytes) * x_scale.astype(np.float64), a, w, d)

@@ -1,0 +1,333 @@
+from contextlib import ExitStack
+
+import concourse.mybir as mybir
+from concourse.masks import make_identity
+
+S, K, M = 1024, 1024, 1024
+FLOPS = 2 * 2 * S * K * M
+
+F32 = mybir.dt.float32
+BF16 = mybir.dt.bfloat16
+U32 = mybir.dt.uint32
+U8 = mybir.dt.uint8
+FP8 = mybir.dt.float8_e4m3fn
+FP8X4 = mybir.dt.float8_e4m3fn_x4
+ALU = mybir.AluOpType
+ACT = mybir.ActivationFunctionType
+
+P = 128
+PACK = 4
+PASS = P * PACK
+PASSES = 2
+BANK = 512
+CHUNKS = [256, 256, 256, 128, 128]
+EPS = 1e-6
+LEAD = 5
+SUM_LAG = 2
+OUT_LAG = 1
+
+
+def tile_weightedsignedsquarepowerstep_kernel(tc, x_bytes, x_scale, a, w, d, out):
+    nc = tc.nc
+    with ExitStack() as ctx:
+        keep = ctx.enter_context(tc.tile_pool(name="keep", bufs=1))
+        work = ctx.enter_context(tc.tile_pool(name="work", bufs=3))
+        psum = ctx.enter_context(tc.psum_pool(name="psum", bufs=1))
+        ctx.enter_context(nc.allow_non_contiguous_dma(reason="small vectors in runs of four"))
+        ctx.enter_context(tc.manual_schedule())
+
+        def kept(name, shape, dtype):
+            return keep.tile(shape, dtype, name=name, align_bytes=64)
+
+        turns = {}
+
+        def bank(ring, dtype=F32):
+            n = turns.get(ring, 0)
+            turns[ring] = n + 1
+            width = BANK if dtype == F32 else 2 * BANK
+            return psum.tile([P, width], dtype, name="bank", tag="bank%d" % ring[n % len(ring)])
+
+        HEAD_RING = (2, 3, 4, 5, 6, 7)
+        Y_RING = (0, 1)
+        T_RING = (2, 3, 4)
+        O_RING = (5, 6, 7)
+        TAIL_RING = (0, 1, 5, 6, 7)
+
+        starts = [sum(CHUNKS[:c]) for c in range(len(CHUNKS))]
+        tiles = [(c, jj) for c, width in enumerate(CHUNKS) for jj in range(width // P)]
+        units = [(c, n) for c, width in enumerate(CHUNKS) for n in range(2 * width // P)]
+
+        xs_col = kept("xs_col", [P, PASSES, PACK], F32)
+        w_col = kept("w_col", [P, PASSES, PACK], BF16)
+        d_col = kept("d_col", [P, PASSES, PACK], BF16)
+        xbytes = [kept("xbytes%d" % c, [P, width // P, K], U8) for c, width in enumerate(CHUNKS)]
+        a_rows = [[kept("a_rows%d%d" % (g, h), [P, 2, K], BF16) for h in range(2)] for g in range(PASSES)]
+
+        def load_x(c):
+            rows = x_bytes[starts[c] : starts[c] + CHUNKS[c], :]
+            nc.sync.dma_start(out=xbytes[c][:], in_=rows.rearrange("(p j) k -> p j k", p=P))
+
+        def load_a(g, h):
+            rows = a[g * PASS : (g + 1) * PASS, :].rearrange("(p t) k -> p t k", t=PACK)
+            nc.sync.dma_start(out=a_rows[g][h][:], in_=rows[:, 2 * h : 2 * h + 2, :])
+
+        nc.sync.dma_start(out=xs_col[:], in_=x_scale.rearrange("o (g p t) -> p (o g) t", g=PASSES, t=PACK))
+        nc.sync.dma_start(out=w_col[:], in_=w.rearrange("(g p t) -> p g t", g=PASSES, t=PACK))
+        load_a(0, 0)
+        load_x(0)
+        load_a(0, 1)
+        load_a(1, 0)
+        load_a(1, 1)
+        load_x(1)
+        nc.sync.dma_start(out=d_col[:], in_=d.rearrange("(g p t) -> p g t", g=PASSES, t=PACK))
+        for c in range(2, len(CHUNKS)):
+            load_x(c)
+
+        def a_slot(g, t):
+            return a_rows[g][t // 2][:, t % 2, :]
+
+        ident = kept("ident", [P, P], F32)
+        make_identity(nc, ident[:])
+        one = kept("one", [P, 1], F32)
+        nc.gpsimd.memset(one[:], 1.0)
+        expo = kept("expo", [P, 1], F32)
+        nc.gpsimd.tensor_scalar(out=expo[:], in0=one[:], scalar1=-2.0 / 3.0, scalar2=0.0, op0=ALU.mult, op1=ALU.add)
+        warm = kept("warm", [P, 1], F32)
+        nc.scalar.activation(out=warm[:], in_=one[:], func=ACT.Abs)
+
+        xs_all = kept("xs_all", [P, K], F32)
+        for g in range(PASSES):
+            b = bank(HEAD_RING)
+            for t in range(PACK):
+                nc.tensor.transpose(b[:, t * P : (t + 1) * P], xs_col[:, g, t : t + 1].to_broadcast([P, P]), ident[:])
+            src = b[:].rearrange("c (t p) -> c p t", t=PACK)
+            dst = xs_all[:, g * PASS : (g + 1) * PASS].rearrange("c (p t) -> c p t", t=PACK)
+            if g == 0:
+                nc.vector.tensor_copy(out=dst, in_=src)
+            else:
+                nc.scalar.copy(out=dst, in_=src)
+
+        w_f32 = kept("w_f32", [P, PASSES * PACK], F32)
+        d_f32 = kept("d_f32", [P, PASSES * PACK], F32)
+        half_sign = kept("half_sign", [P, PASSES * PACK], F32)
+        signs = kept("signs", [P, PASSES * PACK, P], BF16)
+
+        def prepare_w():
+            nc.vector.tensor_copy(out=w_f32[:], in_=w_col[:].rearrange("p g t -> p (g t)"))
+            nc.vector.tensor_scalar(out=half_sign[:], in0=w_col[:].rearrange("p g t -> p (g t)"), scalar1=0.0, scalar2=-0.5, op0=ALU.is_ge, op1=ALU.add)
+            for i in range(PASSES * PACK):
+                nc.vector.tensor_scalar(out=signs[:, i, :], in0=ident[:], scalar1=half_sign[:, i : i + 1], scalar2=2.0, op0=ALU.mult, op1=ALU.mult)
+
+        def prepare_d():
+            nc.vector.tensor_copy(out=d_f32[:], in_=d_col[:].rearrange("p g t -> p (g t)"))
+
+        def quantize(name, grouped, words):
+            codes = kept(name + "_codes", [P, words], U32)
+            scales = kept(name + "_scales", [P, words], U8)
+            nc.vector.quantize_mx(out=codes[:].bitcast(FP8X4), scales=scales[:], in_=grouped)
+            return codes, scales
+
+        def mx(dst, lhs, lhs_cols, rhs, rhs_cols, g):
+            nc.tensor.matmul_mx(
+                out=dst,
+                lhsT=lhs[0][:, lhs_cols].bitcast(FP8X4),
+                lhsT_scale=lhs[1][:, lhs_cols],
+                rhs=rhs[0][:, rhs_cols].bitcast(FP8X4),
+                rhs_scale=rhs[1][:, rhs_cols],
+                start=(g == 0),
+                stop=(g == PASSES - 1),
+            )
+
+        def cols(i, width=P):
+            return slice(i * width, (i + 1) * width)
+
+        turned = {}
+
+        def turn(key, rows, ring):
+            words = rows.bitcast(F32)
+            b = bank(ring)
+            for g in range(PASSES):
+                for u in range(2):
+                    nc.tensor.transpose(b[:, cols(2 * g + u)], words[:, 256 * g + u : 256 * (g + 1) : 2], ident[:])
+            grouped = work.tile([P, K], BF16, name="grouped", tag="grouped", bufs=4, align_bytes=64)
+            nc.scalar.copy(
+                out=grouped[:].bitcast(F32).rearrange("p (g r u) -> p g r u", g=PASSES, u=2),
+                in_=b[:].rearrange("p (g u r) -> p g r u", g=PASSES, u=2),
+            )
+            turned[key] = grouped
+
+        x_scaled = {}
+        xq, aq1, aq2, uq = {}, {}, {}, {}
+
+        def scale_x(j):
+            c, jj = tiles[j]
+            x_scaled[j] = kept("x_scaled%d" % j, [P, K], BF16)
+            nc.vector.tensor_tensor(out=x_scaled[j][:], in0=xbytes[c][:, jj, :].bitcast(FP8), in1=xs_all[:], op=ALU.mult)
+
+        def turn_x(j, ring):
+            turn(("x", j), x_scaled[j][:], ring)
+
+        def quant_x(j):
+            xq[j] = quantize("xq%d" % j, turned[("x", j)][:], K // PACK)
+
+        def turn_a(i, ring):
+            turn(("a", i), a_slot(i // PACK, i % PACK), ring)
+
+        def quant_a1(i):
+            aq1[i] = quantize("aq1_%d" % i, turned[("a", i)][:], K // PACK)
+
+        a_grouped = {}
+
+        def group_a(gm, q, ring):
+            gk, h = q // 2, q % 2
+            b = bank(ring, BF16)
+            for t in range(PACK):
+                nc.tensor.matmul(b[:, cols(t, 256)], lhsT=signs[:, gm * PACK + t, :], rhs=a_slot(gm, t)[:, cols(q, 256)], start=True, stop=True)
+            if h == 0:
+                a_grouped[gm, gk] = kept("a_grouped%d%d" % (gm, gk), [P, PACK, P, PACK], BF16)
+            nc.scalar.copy(
+                out=a_grouped[gm, gk][:, :, cols(h, 64), :],
+                in_=b[:].rearrange("p (tm pk tk) -> p tk pk tm", tm=PACK, tk=PACK),
+            )
+
+        def quant_a2(gm, gk):
+            aq2[gm, gk] = quantize("aq2_%d%d" % (gm, gk), a_grouped[gm, gk][:].rearrange("p t k m -> p (t k m)"), PASS)
+
+        u_grouped = {}
+
+        def first_stage(n):
+            c, i = units[n]
+            nt = CHUNKS[c] // P
+            gm, jj = i // nt, i % nt
+            j = tiles.index((c, jj))
+            b = bank(Y_RING)
+            for t in range(PACK):
+                for g in range(PASSES):
+                    mx(b[:, cols(t)], aq1[gm * PACK + t], cols(g), xq[j], cols(g), g)
+            wy = work.tile([P, BANK], F32, name="wy", tag="wy")
+            for t in range(PACK):
+                nc.scalar.activation(out=wy[:, cols(t)], in_=b[:, cols(t)], func=ACT.Abs, scale=w_f32[:, gm * PACK + t : gm * PACK + t + 1])
+            if jj == 0:
+                u_grouped[c, gm] = kept("u_grouped%d%d" % (c, gm), [P, CHUNKS[c] * PACK], BF16)
+            nc.vector.tensor_tensor(
+                out=u_grouped[c, gm][:, cols(jj, BANK)].rearrange("p (r i t) -> p r t i", i=4, t=PACK),
+                in0=b[:].rearrange("p (t r i) -> p r t i", t=PACK, i=4),
+                in1=wy[:].rearrange("p (t r i) -> p r t i", t=PACK, i=4),
+                op=ALU.mult,
+            )
+
+        def quant_u(n):
+            c, i = units[n]
+            nt = CHUNKS[c] // P
+            if i % nt == nt - 1:
+                uq[c, i // nt] = quantize("uq%d%d" % (c, i // nt), u_grouped[c, i // nt][:], CHUNKS[c])
+
+        square, cube = {}, {}
+
+        def second_stage(n):
+            c, i = units[n]
+            width = CHUNKS[c]
+            per = BANK // width
+            kts = range(i * per, (i + 1) * per)
+            b = bank(T_RING)
+            for e, kt in enumerate(kts):
+                for g in range(PASSES):
+                    mx(b[:, cols(e, width)], aq2[g, kt // PACK], cols(kt % PACK), uq[c, g], slice(0, width), g)
+            az = work.tile([P, BANK], F32, name="az", tag="az")
+            sq = kept("square%d" % n, [P, BANK], F32)
+            cu = kept("cube%d" % n, [P, BANK], F32)
+            for e, kt in enumerate(kts):
+                nc.scalar.activation(out=az[:, cols(e, width)], in_=b[:, cols(e, width)], func=ACT.Abs, scale=d_f32[:, kt : kt + 1])
+            for src, dst in ((az, sq), (sq, cu)):
+                for e, kt in enumerate(kts):
+                    nc.vector.scalar_tensor_tensor(
+                        out=dst[:, cols(e, width)], in0=b[:, cols(e, width)], scalar=d_f32[:, kt : kt + 1],
+                        in1=src[:, cols(e, width)], op0=ALU.mult, op1=ALU.mult,
+                    )
+            for e, kt in enumerate(kts):
+                square[c, kt] = sq[:, cols(e, width)]
+                cube[c, kt] = cu[:, cols(e, width)]
+
+        inv_norm = {}
+
+        def norm(j, ring):
+            c, jj = tiles[j]
+            b = bank(ring)
+            for kt in range(K // P):
+                nc.tensor.matmul(b[:, :P], lhsT=cube[c, kt][:, cols(jj)], rhs=ident[:], is_transpose=True, start=(kt == 0), stop=(kt == K // P - 1))
+            parts = work.tile([P, P], F32, name="parts", tag="parts")
+            mean = kept("mean%d" % j, [P, 1], F32)
+            nc.scalar.activation(out=parts[:], in_=b[:, :P], func=ACT.Identity, scale=1.0 / K, bias=EPS / P, accum_out=mean[:])
+            inv_norm[j] = kept("inv_norm%d" % j, [P, 1], F32)
+            nc.gpsimd.tensor_tensor(out=inv_norm[j][:], in0=mean[:], in1=expo[:], op=ALU.pow)
+
+        def finish(j, gk, on_vector, ring):
+            c, jj = tiles[j]
+            b = bank(ring)
+            for t in range(PACK):
+                nc.tensor.transpose(b[:, cols(t)], square[c, gk * PACK + t][:, cols(jj)], ident[:])
+            res = work.tile([P, BANK], F32, name="res", tag="res", bufs=6)
+            dst = res[:].rearrange("s (p t) -> s p t", t=PACK)
+            src = b[:].rearrange("s (t p) -> s p t", t=PACK)
+            if on_vector:
+                nc.vector.tensor_scalar(out=dst, in0=src, scalar1=inv_norm[j][:], scalar2=None, op0=ALU.mult)
+            else:
+                nc.scalar.activation(out=dst, in_=src, func=ACT.Copy, scale=inv_norm[j][:])
+            rows = out[starts[c] : starts[c] + CHUNKS[c], :].rearrange("(p j) k -> p j k", p=P)
+            nc.sync.dma_start(out=rows[:, jj, cols(gk, PASS)], in_=res[:])
+
+        R = HEAD_RING
+        prepare_w()
+        turn_a(0, R); scale_x(0)
+        turn_a(1, R); scale_x(1); quant_a1(0); quant_a1(1)
+        turn_a(2, R)
+        turn_x(0, R); quant_a1(2)
+        turn_a(3, R); quant_x(0)
+        group_a(0, 0, R); quant_a1(3); scale_x(2)
+        turn_x(1, R)
+        turn_a(4, R); quant_x(1); scale_x(3)
+        first_stage(0)
+        group_a(0, 1, R); quant_a1(4); prepare_d()
+        turn_a(5, R); quant_a2(0, 0)
+        first_stage(1)
+        turn_a(6, R); quant_a1(5); quant_u(1)
+        turn_a(7, R); quant_a1(6); scale_x(4)
+        group_a(1, 0, R); quant_a1(7); scale_x(5)
+        turn_x(2, R)
+        first_stage(2)
+        group_a(1, 1, R); quant_x(2); scale_x(6)
+        first_stage(3)
+        group_a(0, 2, R); quant_a2(1, 0); quant_u(3)
+        turn_x(3, R); scale_x(7)
+        group_a(0, 3, R); quant_x(3)
+        first_stage(4)
+        group_a(1, 2, R); quant_a2(0, 1)
+        group_a(1, 3, R); quant_a2(1, 1)
+
+        last_unit = {c: n for n, (c, i) in enumerate(units)}
+        normed = []
+        halves = [(j, gk) for j in range(len(tiles)) for gk in range(PASSES)]
+        done = 0
+        late = {1: 4, 2: 5, 3: 6, 4: 7}
+        for step in range(len(units) + 4):
+            tail = step + LEAD >= len(units)
+            ring = TAIL_RING if step + LEAD > len(units) else O_RING
+            j = len(normed)
+            if not tail:
+                first_stage(step + LEAD)
+            if step in late:
+                turn_x(late[step], O_RING)
+            if step < len(units):
+                second_stage(step)
+            if step in late:
+                quant_x(late[step])
+            if not tail:
+                quant_u(step + LEAD)
+            for e in range(2 if tail else 1):
+                if done // 2 < len(normed) and normed[done // 2] + OUT_LAG <= step:
+                    finish(halves[done][0], halves[done][1], step >= 13 and e % 2 == 1, ring)
+                    done = done + 1
+            if j < len(tiles) and last_unit[tiles[j][0]] + (SUM_LAG if step < 15 else 0) <= step:
+                norm(j, ring)
+                normed.append(step)
+        assert done == len(halves)

@@ -22,6 +22,8 @@ PASSES = 2
 BANK = 512
 CHUNKS = [256, 256, 256, 128, 128]
 EPS = 1e-6
+GP_CHUNKS = 0
+WARM0 = 3
 LEAD = 5
 SUM_LAG = 2
 OUT_LAG = 1
@@ -47,7 +49,7 @@ def tile_weightedsignedsquarepowerstep_kernel(tc, x_bytes, x_scale, a, w, d, out
             width = BANK if dtype == F32 else 2 * BANK
             return psum.tile([P, width], dtype, name="bank", tag="bank%d" % ring[n % len(ring)])
 
-        HEAD_RING = (2, 3, 4, 5, 6, 7)
+        HEAD_RING = (4, 5, 6, 7, 2, 3)
         Y_RING = (0, 1)
         T_RING = (2, 3, 4)
         O_RING = (5, 6, 7)
@@ -76,9 +78,9 @@ def tile_weightedsignedsquarepowerstep_kernel(tc, x_bytes, x_scale, a, w, d, out
         load_a(0, 0)
         load_x(0)
         load_a(0, 1)
+        load_x(1)
         load_a(1, 0)
         load_a(1, 1)
-        load_x(1)
         nc.sync.dma_start(out=d_col[:], in_=d.rearrange("(g p t) -> p g t", g=PASSES, t=PACK))
         for c in range(2, len(CHUNKS)):
             load_x(c)
@@ -98,14 +100,13 @@ def tile_weightedsignedsquarepowerstep_kernel(tc, x_bytes, x_scale, a, w, d, out
         xs_all = kept("xs_all", [P, K], F32)
         for g in range(PASSES):
             b = bank(HEAD_RING)
+            for t in range(WARM0 if g == 0 else 0):
+                nc.tensor.matmul(b[:, t % 4 * P : (t % 4 + 1) * P], lhsT=ident[:], rhs=ident[:], start=True, stop=True)
             for t in range(PACK):
                 nc.tensor.transpose(b[:, t * P : (t + 1) * P], xs_col[:, g, t : t + 1].to_broadcast([P, P]), ident[:])
             src = b[:].rearrange("c (t p) -> c p t", t=PACK)
             dst = xs_all[:, g * PASS : (g + 1) * PASS].rearrange("c (p t) -> c p t", t=PACK)
-            if g == 0:
-                nc.vector.tensor_copy(out=dst, in_=src)
-            else:
-                nc.scalar.copy(out=dst, in_=src)
+            nc.scalar.copy(out=dst, in_=src)
 
         w_f32 = kept("w_f32", [P, PASSES * PACK], F32)
         d_f32 = kept("d_f32", [P, PASSES * PACK], F32)
@@ -143,14 +144,16 @@ def tile_weightedsignedsquarepowerstep_kernel(tc, x_bytes, x_scale, a, w, d, out
 
         turned = {}
 
-        def turn(key, rows, ring):
+        def turn(key, rows, ring, warm_cols, on_vector=False):
             words = rows.bitcast(F32)
             b = bank(ring)
+            for i in range(warm_cols // P):
+                nc.tensor.matmul(b[:, cols(i)], lhsT=ident[:], rhs=ident[:], start=True, stop=True)
             for g in range(PASSES):
                 for u in range(2):
                     nc.tensor.transpose(b[:, cols(2 * g + u)], words[:, 256 * g + u : 256 * (g + 1) : 2], ident[:])
             grouped = work.tile([P, K], BF16, name="grouped", tag="grouped", bufs=4, align_bytes=64)
-            nc.scalar.copy(
+            (nc.vector.tensor_copy if on_vector else nc.scalar.copy)(
                 out=grouped[:].bitcast(F32).rearrange("p (g r u) -> p g r u", g=PASSES, u=2),
                 in_=b[:].rearrange("p (g u r) -> p g r u", g=PASSES, u=2),
             )
@@ -164,14 +167,14 @@ def tile_weightedsignedsquarepowerstep_kernel(tc, x_bytes, x_scale, a, w, d, out
             x_scaled[j] = kept("x_scaled%d" % j, [P, K], BF16)
             nc.vector.tensor_tensor(out=x_scaled[j][:], in0=xbytes[c][:, jj, :].bitcast(FP8), in1=xs_all[:], op=ALU.mult)
 
-        def turn_x(j, ring):
-            turn(("x", j), x_scaled[j][:], ring)
+        def turn_x(j, ring, warm_cols=0, on_vector=False):
+            turn(("x", j), x_scaled[j][:], ring, warm_cols, on_vector)
 
         def quant_x(j):
             xq[j] = quantize("xq%d" % j, turned[("x", j)][:], K // PACK)
 
-        def turn_a(i, ring):
-            turn(("a", i), a_slot(i // PACK, i % PACK), ring)
+        def turn_a(i, ring, warm_cols=0):
+            turn(("a", i), a_slot(i // PACK, i % PACK), ring, warm_cols)
 
         def quant_a1(i):
             aq1[i] = quantize("aq1_%d" % i, turned[("a", i)][:], K // PACK)
@@ -224,7 +227,7 @@ def tile_weightedsignedsquarepowerstep_kernel(tc, x_bytes, x_scale, a, w, d, out
 
         square, cube = {}, {}
 
-        def second_stage(n):
+        def second_stage(n, between):
             c, i = units[n]
             width = CHUNKS[c]
             per = BANK // width
@@ -239,6 +242,8 @@ def tile_weightedsignedsquarepowerstep_kernel(tc, x_bytes, x_scale, a, w, d, out
             for e, kt in enumerate(kts):
                 nc.scalar.activation(out=az[:, cols(e, width)], in_=b[:, cols(e, width)], func=ACT.Abs, scale=d_f32[:, kt : kt + 1])
             for src, dst in ((az, sq), (sq, cu)):
+                if dst is cu:
+                    between()
                 for e, kt in enumerate(kts):
                     nc.vector.scalar_tensor_tensor(
                         out=dst[:, cols(e, width)], in0=b[:, cols(e, width)], scalar=d_f32[:, kt : kt + 1],
@@ -246,15 +251,19 @@ def tile_weightedsignedsquarepowerstep_kernel(tc, x_bytes, x_scale, a, w, d, out
                     )
             for e, kt in enumerate(kts):
                 square[c, kt] = sq[:, cols(e, width)]
-                cube[c, kt] = cu[:, cols(e, width)]
+            if i > 0 and c < GP_CHUNKS:
+                nc.gpsimd.tensor_tensor(out=cu[:], in0=cu[:], in1=cube[c][0], op=ALU.add)
+                cube[c] = []
+            cube.setdefault(c, []).append(cu[:])
 
         inv_norm = {}
 
         def norm(j, ring):
             c, jj = tiles[j]
             b = bank(ring)
-            for kt in range(K // P):
-                nc.tensor.matmul(b[:, :P], lhsT=cube[c, kt][:, cols(jj)], rhs=ident[:], is_transpose=True, start=(kt == 0), stop=(kt == K // P - 1))
+            blocks = [part[:, e * CHUNKS[c] + jj * P : e * CHUNKS[c] + (jj + 1) * P] for part in cube[c] for e in range(BANK // CHUNKS[c])]
+            for e, block in enumerate(blocks):
+                nc.tensor.matmul(b[:, :P], lhsT=block, rhs=ident[:], is_transpose=True, start=(e == 0), stop=(e == len(blocks) - 1))
             parts = work.tile([P, P], F32, name="parts", tag="parts")
             mean = kept("mean%d" % j, [P, 1], F32)
             nc.scalar.activation(out=parts[:], in_=b[:, :P], func=ACT.Identity, scale=1.0 / K, bias=EPS / P, accum_out=mean[:])
@@ -276,58 +285,68 @@ def tile_weightedsignedsquarepowerstep_kernel(tc, x_bytes, x_scale, a, w, d, out
             rows = out[starts[c] : starts[c] + CHUNKS[c], :].rearrange("(p j) k -> p j k", p=P)
             nc.sync.dma_start(out=rows[:, jj, cols(gk, PASS)], in_=res[:])
 
-        R = HEAD_RING
         prepare_w()
-        turn_a(0, R); scale_x(0)
+        R = HEAD_RING
+        turn_a(0, R, 256); scale_x(0)
         turn_a(1, R); scale_x(1); quant_a1(0); quant_a1(1)
+        turn_x(0, R, 256); scale_x(2)
+        group_a(0, 0, R); quant_x(0); scale_x(3)
         turn_a(2, R)
-        turn_x(0, R); quant_a1(2)
-        turn_a(3, R); quant_x(0)
-        group_a(0, 0, R); quant_a1(3); scale_x(2)
-        turn_x(1, R)
-        turn_a(4, R); quant_x(1); scale_x(3)
-        first_stage(0)
-        group_a(0, 1, R); quant_a1(4); prepare_d()
-        turn_a(5, R); quant_a2(0, 0)
-        first_stage(1)
-        turn_a(6, R); quant_a1(5); quant_u(1)
-        turn_a(7, R); quant_a1(6); scale_x(4)
-        group_a(1, 0, R); quant_a1(7); scale_x(5)
-        turn_x(2, R)
-        first_stage(2)
-        group_a(1, 1, R); quant_x(2); scale_x(6)
+        turn_a(3, R); quant_a1(2)
+        turn_x(1, R); quant_a1(3); scale_x(4)
+        group_a(0, 1, R); quant_x(1); prepare_d()
+        first_stage(0); quant_a2(0, 0)
+        turn_a(4, R)
+        first_stage(1); quant_a1(4); scale_x(5); quant_u(1)
+        turn_a(5, R)
+        group_a(1, 0, R); quant_a1(5)
+        turn_a(6, R); scale_x(6)
+        turn_a(7, R); quant_a1(6)
+        group_a(1, 1, R); quant_a1(7); scale_x(7)
+        turn_x(2, R); quant_a2(1, 0)
+        turn_x(3, R, 0, True); quant_x(2)
+        first_stage(2); quant_x(3)
+        group_a(0, 2, R)
         first_stage(3)
-        group_a(0, 2, R); quant_a2(1, 0); quant_u(3)
-        turn_x(3, R); scale_x(7)
-        group_a(0, 3, R); quant_x(3)
-        first_stage(4)
-        group_a(1, 2, R); quant_a2(0, 1)
+        group_a(0, 3, R); quant_u(3)
+        first_stage(4); quant_a2(0, 1)
+        group_a(1, 2, R)
         group_a(1, 3, R); quant_a2(1, 1)
 
         last_unit = {c: n for n, (c, i) in enumerate(units)}
         normed = []
         halves = [(j, gk) for j in range(len(tiles)) for gk in range(PASSES)]
         done = 0
-        late = {1: 4, 2: 5, 3: 6, 4: 7}
+        late = {0: 4, 1: 5, 3: 6, 4: 7}
+        late_a = {}
         for step in range(len(units) + 4):
             tail = step + LEAD >= len(units)
             ring = TAIL_RING if step + LEAD > len(units) else O_RING
-            j = len(normed)
+
+            def quantise():
+                if step - 1 in late:
+                    quant_x(late[step - 1])
+                if late_a.get(step - 1, 0) % 2 == 1:
+                    quant_a2(1, 1)
+                if not tail:
+                    quant_u(step + LEAD)
+
             if not tail:
                 first_stage(step + LEAD)
+            if step < len(units):
+                second_stage(step, quantise)
+
+            if step in late_a:
+                group_a(1, late_a[step], O_RING)
             if step in late:
                 turn_x(late[step], O_RING)
-            if step < len(units):
-                second_stage(step)
-            if step in late:
-                quant_x(late[step])
-            if not tail:
-                quant_u(step + LEAD)
             for e in range(2 if tail else 1):
                 if done // 2 < len(normed) and normed[done // 2] + OUT_LAG <= step:
-                    finish(halves[done][0], halves[done][1], step >= 13 and e % 2 == 1, ring)
+                    finish(halves[done][0], halves[done][1], step >= 14 and e % 2 == 1, ring)
                     done = done + 1
-            if j < len(tiles) and last_unit[tiles[j][0]] + (SUM_LAG if step < 15 else 0) <= step:
-                norm(j, ring)
-                normed.append(step)
+            for e in range(2 if step >= 99 else 1):
+                j = len(normed)
+                if j < len(tiles) and last_unit[tiles[j][0]] + (SUM_LAG if step < 15 else 0) <= step:
+                    norm(j, ring)
+                    normed.append(step)
         assert done == len(halves)

@@ -20,13 +20,11 @@ PACK = 4
 PASS = P * PACK
 PASSES = 2
 BANK = 512
-CHUNKS = [256, 256, 256, 128, 128]
+TILES = S // P
+UNITS = TILES * PASSES
 EPS = 1e-6
-GP_CHUNKS = 0
-WARM0 = 3
-LEAD = 5
-SUM_LAG = 2
-OUT_LAG = 1
+LEAD = 4
+BACK_LAG = 2
 
 
 def tile_weightedsignedsquarepowerstep_kernel(tc, x_bytes, x_scale, a, w, d, out):
@@ -49,41 +47,33 @@ def tile_weightedsignedsquarepowerstep_kernel(tc, x_bytes, x_scale, a, w, d, out
             width = BANK if dtype == F32 else 2 * BANK
             return psum.tile([P, width], dtype, name="bank", tag="bank%d" % ring[n % len(ring)])
 
-        HEAD_RING = (4, 5, 6, 7, 2, 3)
+        HEAD_RING = (3, 4, 5, 6, 7, 2)
         Y_RING = (0, 1)
-        T_RING = (2, 3, 4)
-        O_RING = (5, 6, 7)
-        TAIL_RING = (0, 1, 5, 6, 7)
+        T_RING = (2, 3)
+        Z_RING = (4, 5, 6, 7)
 
-        starts = [sum(CHUNKS[:c]) for c in range(len(CHUNKS))]
-        tiles = [(c, jj) for c, width in enumerate(CHUNKS) for jj in range(width // P)]
-        units = [(c, n) for c, width in enumerate(CHUNKS) for n in range(2 * width // P)]
+        def cols(i, width=P):
+            return slice(i * width, (i + 1) * width)
 
         xs_col = kept("xs_col", [P, PASSES, PACK], F32)
         w_col = kept("w_col", [P, PASSES, PACK], BF16)
         d_col = kept("d_col", [P, PASSES, PACK], BF16)
-        xbytes = [kept("xbytes%d" % c, [P, width // P, K], U8) for c, width in enumerate(CHUNKS)]
+        xbytes = [kept("xbytes%d" % c, [P, 2, K], U8) for c in range(TILES // 2)]
         a_rows = [[kept("a_rows%d%d" % (g, h), [P, 2, K], BF16) for h in range(2)] for g in range(PASSES)]
 
         def load_x(c):
-            rows = x_bytes[starts[c] : starts[c] + CHUNKS[c], :]
-            nc.sync.dma_start(out=xbytes[c][:], in_=rows.rearrange("(p j) k -> p j k", p=P))
+            nc.sync.dma_start(out=xbytes[c][:], in_=x_bytes[cols(c, 2 * P), :].rearrange("(p j) k -> p j k", j=2))
 
         def load_a(g, h):
-            rows = a[g * PASS : (g + 1) * PASS, :].rearrange("(p t) k -> p t k", t=PACK)
+            rows = a[cols(g, PASS), :].rearrange("(p t) k -> p t k", t=PACK)
             nc.sync.dma_start(out=a_rows[g][h][:], in_=rows[:, 2 * h : 2 * h + 2, :])
 
         nc.sync.dma_start(out=xs_col[:], in_=x_scale.rearrange("o (g p t) -> p (o g) t", g=PASSES, t=PACK))
         nc.sync.dma_start(out=w_col[:], in_=w.rearrange("(g p t) -> p g t", g=PASSES, t=PACK))
-        load_a(0, 0)
-        load_x(0)
-        load_a(0, 1)
-        load_x(1)
-        load_a(1, 0)
-        load_a(1, 1)
+        load_a(0, 0); load_x(0); load_a(0, 1); load_x(1); load_a(1, 0); load_a(1, 1)
         nc.sync.dma_start(out=d_col[:], in_=d.rearrange("(g p t) -> p g t", g=PASSES, t=PACK))
-        for c in range(2, len(CHUNKS)):
-            load_x(c)
+        load_x(2)
+        load_x(3)
 
         def a_slot(g, t):
             return a_rows[g][t // 2][:, t % 2, :]
@@ -97,27 +87,29 @@ def tile_weightedsignedsquarepowerstep_kernel(tc, x_bytes, x_scale, a, w, d, out
         warm = kept("warm", [P, 1], F32)
         nc.scalar.activation(out=warm[:], in_=one[:], func=ACT.Abs)
 
-        xs_all = kept("xs_all", [P, K], F32)
-        for g in range(PASSES):
-            b = bank(HEAD_RING)
-            for t in range(WARM0 if g == 0 else 0):
-                nc.tensor.matmul(b[:, t % 4 * P : (t % 4 + 1) * P], lhsT=ident[:], rhs=ident[:], start=True, stop=True)
-            for t in range(PACK):
-                nc.tensor.transpose(b[:, t * P : (t + 1) * P], xs_col[:, g, t : t + 1].to_broadcast([P, P]), ident[:])
-            src = b[:].rearrange("c (t p) -> c p t", t=PACK)
-            dst = xs_all[:, g * PASS : (g + 1) * PASS].rearrange("c (p t) -> c p t", t=PACK)
-            nc.scalar.copy(out=dst, in_=src)
+        def warm_up(b, count):
+            for i in range(count):
+                nc.tensor.matmul(b[:, cols(i)], lhsT=ident[:], rhs=ident[:], start=True, stop=True)
 
         w_f32 = kept("w_f32", [P, PASSES * PACK], F32)
         d_f32 = kept("d_f32", [P, PASSES * PACK], F32)
         half_sign = kept("half_sign", [P, PASSES * PACK], F32)
         signs = kept("signs", [P, PASSES * PACK, P], BF16)
+        nc.vector.tensor_copy(out=w_f32[:], in_=w_col[:].rearrange("p g t -> p (g t)"))
+        nc.vector.tensor_scalar(out=half_sign[:], in0=w_col[:].rearrange("p g t -> p (g t)"), scalar1=0.0, scalar2=-0.5, op0=ALU.is_ge, op1=ALU.add)
+        for i in range(PASSES * PACK):
+            nc.vector.tensor_scalar(out=signs[:, i, :], in0=ident[:], scalar1=half_sign[:, i : i + 1], scalar2=2.0, op0=ALU.mult, op1=ALU.mult)
 
-        def prepare_w():
-            nc.vector.tensor_copy(out=w_f32[:], in_=w_col[:].rearrange("p g t -> p (g t)"))
-            nc.vector.tensor_scalar(out=half_sign[:], in0=w_col[:].rearrange("p g t -> p (g t)"), scalar1=0.0, scalar2=-0.5, op0=ALU.is_ge, op1=ALU.add)
-            for i in range(PASSES * PACK):
-                nc.vector.tensor_scalar(out=signs[:, i, :], in0=ident[:], scalar1=half_sign[:, i : i + 1], scalar2=2.0, op0=ALU.mult, op1=ALU.mult)
+        xs_all = kept("xs_all", [P, K], F32)
+        for g in range(PASSES):
+            b = bank(HEAD_RING)
+            warm_up(b, 3 if g == 0 else 0)
+            for t in range(PACK):
+                nc.tensor.transpose(b[:, cols(t)], xs_col[:, g, t : t + 1].to_broadcast([P, P]), ident[:])
+            (nc.vector.tensor_copy if g == 9 else nc.scalar.copy)(
+                out=xs_all[:, cols(g, PASS)].rearrange("c (p t) -> c p t", t=PACK),
+                in_=b[:].rearrange("c (t p) -> c p t", t=PACK),
+            )
 
         def prepare_d():
             nc.vector.tensor_copy(out=d_f32[:], in_=d_col[:].rearrange("p g t -> p (g t)"))
@@ -139,16 +131,12 @@ def tile_weightedsignedsquarepowerstep_kernel(tc, x_bytes, x_scale, a, w, d, out
                 stop=(g == PASSES - 1),
             )
 
-        def cols(i, width=P):
-            return slice(i * width, (i + 1) * width)
-
         turned = {}
 
-        def turn(key, rows, ring, warm_cols, on_vector=False):
+        def turn(key, rows, ring, warm_count, on_vector):
             words = rows.bitcast(F32)
             b = bank(ring)
-            for i in range(warm_cols // P):
-                nc.tensor.matmul(b[:, cols(i)], lhsT=ident[:], rhs=ident[:], start=True, stop=True)
+            warm_up(b, warm_count)
             for g in range(PASSES):
                 for u in range(2):
                     nc.tensor.transpose(b[:, cols(2 * g + u)], words[:, 256 * g + u : 256 * (g + 1) : 2], ident[:])
@@ -163,32 +151,31 @@ def tile_weightedsignedsquarepowerstep_kernel(tc, x_bytes, x_scale, a, w, d, out
         xq, aq1, aq2, uq = {}, {}, {}, {}
 
         def scale_x(j):
-            c, jj = tiles[j]
             x_scaled[j] = kept("x_scaled%d" % j, [P, K], BF16)
-            nc.vector.tensor_tensor(out=x_scaled[j][:], in0=xbytes[c][:, jj, :].bitcast(FP8), in1=xs_all[:], op=ALU.mult)
+            nc.vector.tensor_tensor(out=x_scaled[j][:], in0=xbytes[j // 2][:, j % 2, :].bitcast(FP8), in1=xs_all[:], op=ALU.mult)
 
-        def turn_x(j, ring, warm_cols=0, on_vector=False):
-            turn(("x", j), x_scaled[j][:], ring, warm_cols, on_vector)
+        def turn_x(j, ring, warm_count=0, on_vector=False):
+            turn(("x", j), x_scaled[j][:], ring, warm_count, on_vector)
 
         def quant_x(j):
             xq[j] = quantize("xq%d" % j, turned[("x", j)][:], K // PACK)
 
-        def turn_a(i, ring, warm_cols=0):
-            turn(("a", i), a_slot(i // PACK, i % PACK), ring, warm_cols)
+        def turn_a(i, ring, warm_count=0, on_vector=False):
+            turn(("a", i), a_slot(i // PACK, i % PACK), ring, warm_count, on_vector)
 
         def quant_a1(i):
             aq1[i] = quantize("aq1_%d" % i, turned[("a", i)][:], K // PACK)
 
         a_grouped = {}
 
-        def group_a(gm, q, ring):
+        def group_a(gm, q, ring, on_vector=False):
             gk, h = q // 2, q % 2
             b = bank(ring, BF16)
             for t in range(PACK):
                 nc.tensor.matmul(b[:, cols(t, 256)], lhsT=signs[:, gm * PACK + t, :], rhs=a_slot(gm, t)[:, cols(q, 256)], start=True, stop=True)
             if h == 0:
                 a_grouped[gm, gk] = kept("a_grouped%d%d" % (gm, gk), [P, PACK, P, PACK], BF16)
-            nc.scalar.copy(
+            (nc.vector.tensor_copy if on_vector else nc.scalar.copy)(
                 out=a_grouped[gm, gk][:, :, cols(h, 64), :],
                 in_=b[:].rearrange("p (tm pk tk) -> p tk pk tm", tm=PACK, tk=PACK),
             )
@@ -199,10 +186,7 @@ def tile_weightedsignedsquarepowerstep_kernel(tc, x_bytes, x_scale, a, w, d, out
         u_grouped = {}
 
         def first_stage(n):
-            c, i = units[n]
-            nt = CHUNKS[c] // P
-            gm, jj = i // nt, i % nt
-            j = tiles.index((c, jj))
+            j, gm = n // PASSES, n % PASSES
             b = bank(Y_RING)
             for t in range(PACK):
                 for g in range(PASSES):
@@ -210,86 +194,75 @@ def tile_weightedsignedsquarepowerstep_kernel(tc, x_bytes, x_scale, a, w, d, out
             wy = work.tile([P, BANK], F32, name="wy", tag="wy")
             for t in range(PACK):
                 nc.scalar.activation(out=wy[:, cols(t)], in_=b[:, cols(t)], func=ACT.Abs, scale=w_f32[:, gm * PACK + t : gm * PACK + t + 1])
-            if jj == 0:
-                u_grouped[c, gm] = kept("u_grouped%d%d" % (c, gm), [P, CHUNKS[c] * PACK], BF16)
+            if gm == 0:
+                u_grouped[j] = kept("u_grouped%d" % j, [P, M], BF16)
             nc.vector.tensor_tensor(
-                out=u_grouped[c, gm][:, cols(jj, BANK)].rearrange("p (r i t) -> p r t i", i=4, t=PACK),
+                out=u_grouped[j][:, cols(gm, PASS)].rearrange("p (r i t) -> p r t i", i=4, t=PACK),
                 in0=b[:].rearrange("p (t r i) -> p r t i", t=PACK, i=4),
                 in1=wy[:].rearrange("p (t r i) -> p r t i", t=PACK, i=4),
                 op=ALU.mult,
             )
 
-        def quant_u(n):
-            c, i = units[n]
-            nt = CHUNKS[c] // P
-            if i % nt == nt - 1:
-                uq[c, i // nt] = quantize("uq%d%d" % (c, i // nt), u_grouped[c, i // nt][:], CHUNKS[c])
+        def quant_u(j):
+            uq[j] = quantize("uq%d" % j, u_grouped[j][:], M // PACK)
 
-        square, cube = {}, {}
+        z_cols = {}
 
-        def second_stage(n, between):
-            c, i = units[n]
-            width = CHUNKS[c]
-            per = BANK // width
-            kts = range(i * per, (i + 1) * per)
+        def second_stage(n):
+            j, gk = n // PASSES, n % PASSES
             b = bank(T_RING)
-            for e, kt in enumerate(kts):
-                for g in range(PASSES):
-                    mx(b[:, cols(e, width)], aq2[g, kt // PACK], cols(kt % PACK), uq[c, g], slice(0, width), g)
-            az = work.tile([P, BANK], F32, name="az", tag="az")
-            sq = kept("square%d" % n, [P, BANK], F32)
-            cu = kept("cube%d" % n, [P, BANK], F32)
-            for e, kt in enumerate(kts):
-                nc.scalar.activation(out=az[:, cols(e, width)], in_=b[:, cols(e, width)], func=ACT.Abs, scale=d_f32[:, kt : kt + 1])
-            for src, dst in ((az, sq), (sq, cu)):
-                if dst is cu:
-                    between()
-                for e, kt in enumerate(kts):
-                    nc.vector.scalar_tensor_tensor(
-                        out=dst[:, cols(e, width)], in0=b[:, cols(e, width)], scalar=d_f32[:, kt : kt + 1],
-                        in1=src[:, cols(e, width)], op0=ALU.mult, op1=ALU.mult,
-                    )
-            for e, kt in enumerate(kts):
-                square[c, kt] = sq[:, cols(e, width)]
-            if i > 0 and c < GP_CHUNKS:
-                nc.gpsimd.tensor_tensor(out=cu[:], in0=cu[:], in1=cube[c][0], op=ALU.add)
-                cube[c] = []
-            cube.setdefault(c, []).append(cu[:])
-
-        inv_norm = {}
-
-        def norm(j, ring):
-            c, jj = tiles[j]
-            b = bank(ring)
-            blocks = [part[:, e * CHUNKS[c] + jj * P : e * CHUNKS[c] + (jj + 1) * P] for part in cube[c] for e in range(BANK // CHUNKS[c])]
-            for e, block in enumerate(blocks):
-                nc.tensor.matmul(b[:, :P], lhsT=block, rhs=ident[:], is_transpose=True, start=(e == 0), stop=(e == len(blocks) - 1))
-            parts = work.tile([P, P], F32, name="parts", tag="parts")
-            mean = kept("mean%d" % j, [P, 1], F32)
-            nc.scalar.activation(out=parts[:], in_=b[:, :P], func=ACT.Identity, scale=1.0 / K, bias=EPS / P, accum_out=mean[:])
-            inv_norm[j] = kept("inv_norm%d" % j, [P, 1], F32)
-            nc.gpsimd.tensor_tensor(out=inv_norm[j][:], in0=mean[:], in1=expo[:], op=ALU.pow)
-
-        def finish(j, gk, on_vector, ring):
-            c, jj = tiles[j]
-            b = bank(ring)
             for t in range(PACK):
-                nc.tensor.transpose(b[:, cols(t)], square[c, gk * PACK + t][:, cols(jj)], ident[:])
-            res = work.tile([P, BANK], F32, name="res", tag="res", bufs=6)
-            dst = res[:].rearrange("s (p t) -> s p t", t=PACK)
-            src = b[:].rearrange("s (t p) -> s p t", t=PACK)
-            if on_vector:
-                nc.vector.tensor_scalar(out=dst, in0=src, scalar1=inv_norm[j][:], scalar2=None, op0=ALU.mult)
-            else:
-                nc.scalar.activation(out=dst, in_=src, func=ACT.Copy, scale=inv_norm[j][:])
-            rows = out[starts[c] : starts[c] + CHUNKS[c], :].rearrange("(p j) k -> p j k", p=P)
-            nc.sync.dma_start(out=rows[:, jj, cols(gk, PASS)], in_=res[:])
+                for g in range(PASSES):
+                    mx(b[:, cols(t)], aq2[g, gk], cols(t), uq[j], cols(g), g)
+            z_cols[n] = work.tile([P, BANK], F32, name="z", tag="z", bufs=4)
+            for t in range(PACK):
+                nc.scalar.activation(out=z_cols[n][:, cols(t)], in_=b[:, cols(t)], func=ACT.Copy, scale=d_f32[:, gk * PACK + t : gk * PACK + t + 1])
 
-        prepare_w()
+        z_rows, square, cube_sum = {}, {}, {}
+
+        def signed_square(n):
+            b = bank(Z_RING)
+            for t in range(PACK):
+                nc.tensor.transpose(b[:, cols(t)], z_cols[n][:, cols(t)], ident[:])
+            z_rows[n] = b[:].rearrange("s (t p) -> s p t", t=PACK)
+            az = work.tile([P, P, PACK], F32, name="az", tag="az")
+            nc.scalar.activation(out=az[:], in_=z_rows[n], func=ACT.Abs)
+            square[n] = work.tile([P, P, PACK], F32, name="sq", tag="sq", bufs=8)
+            nc.vector.tensor_tensor(out=square[n][:], in0=z_rows[n], in1=az[:], op=ALU.mult)
+
+        def cube(n):
+            cu = work.tile([P, P, PACK], F32, name="cu", tag="cu", bufs=2)
+            cube_sum[n] = kept("cube_sum%d" % n, [P, 1], F32)
+            nc.vector.scalar_tensor_tensor(out=cu[:], in0=z_rows[n], scalar=1.0 / K, in1=square[n][:], op0=ALU.mult, op1=ALU.mult, accum_out=cube_sum[n][:])
+
+        inv_norms = {}
+
+        def norm(j):
+            mean = kept("mean%d" % j, [P, 1], F32)
+            (nc.vector if j == TILES - 1 else nc.gpsimd).tensor_scalar(out=mean[:], in0=cube_sum[2 * j][:], scalar1=cube_sum[2 * j + 1][:], scalar2=EPS, op0=ALU.add, op1=ALU.add)
+            inv_norm = kept("inv_norm%d" % j, [P, 1], F32)
+            nc.gpsimd.tensor_tensor(out=inv_norm[:], in0=mean[:], in1=expo[:], op=ALU.pow)
+            inv_norms[j] = inv_norm
+
+        def finish(j):
+            last = j >= 5
+            inv_norm = inv_norms[j]
+            rows = out[cols(j // 2, 2 * P), :].rearrange("(p j) k -> p j k", j=2)
+            for gk in range(PASSES):
+                res = work.tile([P, BANK], F32, name="res", tag="res", bufs=8)
+                src = square[2 * j + gk][:].rearrange("s p t -> s (p t)")
+                if not last:
+                    nc.gpsimd.tensor_scalar(out=res[:], in0=src, scalar1=inv_norm[:], scalar2=0.0, op0=ALU.mult, op1=ALU.add)
+                elif gk == 0 or j < TILES - 1:
+                    nc.scalar.activation(out=res[:], in_=src, func=ACT.Copy, scale=inv_norm[:])
+                else:
+                    nc.vector.tensor_scalar(out=res[:], in0=src, scalar1=inv_norm[:], scalar2=None, op0=ALU.mult)
+                nc.sync.dma_start(out=rows[:, j % 2, cols(gk, PASS)], in_=res[:])
+
         R = HEAD_RING
-        turn_a(0, R, 256); scale_x(0)
+        turn_a(0, R, 2); scale_x(0)
         turn_a(1, R); scale_x(1); quant_a1(0); quant_a1(1)
-        turn_x(0, R, 256); scale_x(2)
+        turn_x(0, R, 2); scale_x(2)
         group_a(0, 0, R); quant_x(0); scale_x(3)
         turn_a(2, R)
         turn_a(3, R); quant_a1(2)
@@ -297,56 +270,45 @@ def tile_weightedsignedsquarepowerstep_kernel(tc, x_bytes, x_scale, a, w, d, out
         group_a(0, 1, R); quant_x(1); prepare_d()
         first_stage(0); quant_a2(0, 0)
         turn_a(4, R)
-        first_stage(1); quant_a1(4); scale_x(5); quant_u(1)
+        first_stage(2); quant_a1(4); scale_x(5)
         turn_a(5, R)
         group_a(1, 0, R); quant_a1(5)
         turn_a(6, R); scale_x(6)
         turn_a(7, R); quant_a1(6)
         group_a(1, 1, R); quant_a1(7); scale_x(7)
         turn_x(2, R); quant_a2(1, 0)
-        turn_x(3, R, 0, True); quant_x(2)
-        first_stage(2); quant_x(3)
-        group_a(0, 2, R)
+        group_a(0, 2, R); quant_x(2)
+        turn_x(3, R, 0, True)
+        first_stage(1); quant_x(3)
+        group_a(0, 3, R, True); quant_u(0)
+        group_a(1, 2, R); quant_a2(0, 1)
         first_stage(3)
-        group_a(0, 3, R); quant_u(3)
-        first_stage(4); quant_a2(0, 1)
-        group_a(1, 2, R)
-        group_a(1, 3, R); quant_a2(1, 1)
-
-        last_unit = {c: n for n, (c, i) in enumerate(units)}
-        normed = []
-        halves = [(j, gk) for j in range(len(tiles)) for gk in range(PASSES)]
-        done = 0
-        late = {0: 4, 1: 5, 3: 6, 4: 7}
-        late_a = {}
-        for step in range(len(units) + 4):
-            tail = step + LEAD >= len(units)
-            ring = TAIL_RING if step + LEAD > len(units) else O_RING
-
-            def quantise():
-                if step - 1 in late:
-                    quant_x(late[step - 1])
-                if late_a.get(step - 1, 0) % 2 == 1:
-                    quant_a2(1, 1)
-                if not tail:
-                    quant_u(step + LEAD)
-
-            if not tail:
-                first_stage(step + LEAD)
-            if step < len(units):
-                second_stage(step, quantise)
-
-            if step in late_a:
-                group_a(1, late_a[step], O_RING)
+        group_a(1, 3, R, False); quant_u(1); quant_a2(1, 1)
+        late = {0: 4, 2: 5, 4: 6, 6: 7}
+        late_scale = {}
+        cubed = 0
+        for step in range(UNITS + BACK_LAG + 1):
+            ahead, back = step + LEAD, step - BACK_LAG
+            if 0 <= back < UNITS:
+                signed_square(back)
+            if ahead < UNITS:
+                first_stage(ahead)
+            if step - 1 in late:
+                quant_x(late[step - 1])
+            if cubed < back + (1 if ahead < UNITS else 0):
+                cube(cubed)
+                cubed = cubed + 1
+                if cubed % 2 == 0:
+                    norm(cubed // 2 - 1)
+                    if cubed // 2 <= 5:
+                        finish(cubed // 2 - 1)
+            if ahead % 2 == 1 and ahead < UNITS:
+                quant_u(ahead // 2)
+            if step in late_scale:
+                scale_x(late_scale[step])
+            if step < UNITS:
+                second_stage(step)
             if step in late:
-                turn_x(late[step], O_RING)
-            for e in range(2 if tail else 1):
-                if done // 2 < len(normed) and normed[done // 2] + OUT_LAG <= step:
-                    finish(halves[done][0], halves[done][1], step >= 14 and e % 2 == 1, ring)
-                    done = done + 1
-            for e in range(2 if step >= 99 else 1):
-                j = len(normed)
-                if j < len(tiles) and last_unit[tiles[j][0]] + (SUM_LAG if step < 15 else 0) <= step:
-                    norm(j, ring)
-                    normed.append(step)
-        assert done == len(halves)
+                turn_x(late[step], Z_RING)
+        for j in range(5, TILES):
+            finish(j)

@@ -57,7 +57,7 @@ def tile_weightedsignedsquarepowerstep_kernel(tc, x_bytes, x_scale, a, w, d, out
 
         xs_col = kept("xs_col", [P, PASSES, PACK], F32)
         w_col = kept("w_col", [P, PASSES, PACK], BF16)
-        d_col = kept("d_col", [P, PASSES, PACK], BF16)
+        d_col = kept("d_col", [P, K // P, 2], BF16)
         xbytes = [kept("xbytes%d" % c, [P, 2, K], U8) for c in range(TILES // 2)]
         a_rows = [[kept("a_rows%d%d" % (g, h), [P, 2, K], BF16) for h in range(2)] for g in range(PASSES)]
 
@@ -71,9 +71,9 @@ def tile_weightedsignedsquarepowerstep_kernel(tc, x_bytes, x_scale, a, w, d, out
         nc.sync.dma_start(out=xs_col[:], in_=x_scale.rearrange("o (g p t) -> p (o g) t", g=PASSES, t=PACK))
         nc.sync.dma_start(out=w_col[:], in_=w.rearrange("(g p t) -> p g t", g=PASSES, t=PACK))
         load_a(0, 0); load_x(0); load_a(0, 1); load_x(1); load_a(1, 0); load_a(1, 1)
-        nc.sync.dma_start(out=d_col[:], in_=d.rearrange("(g p t) -> p g t", g=PASSES, t=PACK))
         load_x(2)
         load_x(3)
+        nc.sync.dma_start(out=d_col[:, :, 0], in_=d.rearrange("(j p) -> p j", p=P))
 
         def a_slot(g, t):
             return a_rows[g][t // 2][:, t % 2, :]
@@ -94,11 +94,14 @@ def tile_weightedsignedsquarepowerstep_kernel(tc, x_bytes, x_scale, a, w, d, out
         w_f32 = kept("w_f32", [P, PASSES * PACK], F32)
         d_f32 = kept("d_f32", [P, PASSES * PACK], F32)
         half_sign = kept("half_sign", [P, PASSES * PACK], F32)
-        signs = kept("signs", [P, PASSES * PACK, P], BF16)
+        ident_bf = kept("ident_bf", [P, P], BF16)
+        nc.vector.tensor_copy(out=ident_bf[:], in_=ident[:])
         nc.vector.tensor_copy(out=w_f32[:], in_=w_col[:].rearrange("p g t -> p (g t)"))
         nc.vector.tensor_scalar(out=half_sign[:], in0=w_col[:].rearrange("p g t -> p (g t)"), scalar1=0.0, scalar2=-0.5, op0=ALU.is_ge, op1=ALU.add)
-        for i in range(PASSES * PACK):
-            nc.vector.tensor_scalar(out=signs[:, i, :], in0=ident[:], scalar1=half_sign[:, i : i + 1], scalar2=2.0, op0=ALU.mult, op1=ALU.mult)
+        signed = [kept("signed%d" % g, [P, PACK, K], BF16) for g in range(PASSES)]
+
+        def sign_a(i):
+            nc.vector.tensor_scalar(out=signed[i // PACK][:, i % PACK, :], in0=a_slot(i // PACK, i % PACK), scalar1=half_sign[:, i : i + 1], scalar2=2.0, op0=ALU.mult, op1=ALU.mult)
 
         xs_all = kept("xs_all", [P, K], F32)
         for g in range(PASSES):
@@ -112,7 +115,7 @@ def tile_weightedsignedsquarepowerstep_kernel(tc, x_bytes, x_scale, a, w, d, out
             )
 
         def prepare_d():
-            nc.vector.tensor_copy(out=d_f32[:], in_=d_col[:].rearrange("p g t -> p (g t)"))
+            nc.vector.tensor_copy(out=d_f32[:], in_=d_col[:, :, 0])
 
         def quantize(name, grouped, words):
             codes = kept(name + "_codes", [P, words], U32)
@@ -171,17 +174,14 @@ def tile_weightedsignedsquarepowerstep_kernel(tc, x_bytes, x_scale, a, w, d, out
         def group_a(gm, q, ring, on_vector=False):
             gk, h = q // 2, q % 2
             b = bank(ring, BF16)
-            for t in range(PACK):
-                nc.tensor.matmul(b[:, cols(t, 256)], lhsT=signs[:, gm * PACK + t, :], rhs=a_slot(gm, t)[:, cols(q, 256)], start=True, stop=True)
+            for e in range(2):
+                nc.tensor.matmul(b[:, cols(e, PASS)], lhsT=ident_bf[:], rhs=signed[gm][:, :, cols(2 * q + e)].rearrange("p t k -> p k t"), start=True, stop=True)
             if h == 0:
-                a_grouped[gm, gk] = kept("a_grouped%d%d" % (gm, gk), [P, PACK, P, PACK], BF16)
-            (nc.vector.tensor_copy if on_vector else nc.scalar.copy)(
-                out=a_grouped[gm, gk][:, :, cols(h, 64), :],
-                in_=b[:].rearrange("p (tm pk tk) -> p tk pk tm", tm=PACK, tk=PACK),
-            )
+                a_grouped[gm, gk] = kept("a_grouped%d%d" % (gm, gk), [P, PASS * PACK], BF16)
+            nc.scalar.copy(out=a_grouped[gm, gk][:, cols(h, 2 * PASS)], in_=b[:])
 
         def quant_a2(gm, gk):
-            aq2[gm, gk] = quantize("aq2_%d%d" % (gm, gk), a_grouped[gm, gk][:].rearrange("p t k m -> p (t k m)"), PASS)
+            aq2[gm, gk] = quantize("aq2_%d%d" % (gm, gk), a_grouped[gm, gk][:], PASS)
 
         u_grouped = {}
 
@@ -218,28 +218,30 @@ def tile_weightedsignedsquarepowerstep_kernel(tc, x_bytes, x_scale, a, w, d, out
             for t in range(PACK):
                 nc.scalar.activation(out=z_cols[n][:, cols(t)], in_=b[:, cols(t)], func=ACT.Copy, scale=d_f32[:, gk * PACK + t : gk * PACK + t + 1])
 
-        z_rows, square, cube_sum = {}, {}, {}
+        z_rows, square, squares, cube_sum = {}, {}, {}, {}
 
         def signed_square(n):
             b = bank(Z_RING)
             for t in range(PACK):
                 nc.tensor.transpose(b[:, cols(t)], z_cols[n][:, cols(t)], ident[:])
-            z_rows[n] = b[:].rearrange("s (t p) -> s p t", t=PACK)
-            az = work.tile([P, P, PACK], F32, name="az", tag="az")
+            z_rows[n] = b[:]
+            az = work.tile([P, BANK], F32, name="az", tag="az")
             nc.scalar.activation(out=az[:], in_=z_rows[n], func=ACT.Abs)
-            square[n] = work.tile([P, P, PACK], F32, name="sq", tag="sq", bufs=8)
-            nc.vector.tensor_tensor(out=square[n][:], in0=z_rows[n], in1=az[:], op=ALU.mult)
+            if n % 2 == 0:
+                squares[n // 2] = work.tile([P, K], F32, name="sq", tag="sq", bufs=4)
+            square[n] = squares[n // 2][:, cols(n % 2, PASS)]
+            nc.vector.tensor_tensor(out=square[n], in0=z_rows[n], in1=az[:], op=ALU.mult)
 
         def cube(n):
-            cu = work.tile([P, P, PACK], F32, name="cu", tag="cu", bufs=2)
+            cu = work.tile([P, BANK], F32, name="cu", tag="cu", bufs=2)
             cube_sum[n] = kept("cube_sum%d" % n, [P, 1], F32)
-            nc.vector.scalar_tensor_tensor(out=cu[:], in0=z_rows[n], scalar=1.0 / K, in1=square[n][:], op0=ALU.mult, op1=ALU.mult, accum_out=cube_sum[n][:])
+            nc.vector.scalar_tensor_tensor(out=cu[:], in0=z_rows[n], scalar=1.0 / K, in1=square[n], op0=ALU.mult, op1=ALU.mult, accum_out=cube_sum[n][:])
 
         inv_norms = {}
 
         def norm(j):
             mean = kept("mean%d" % j, [P, 1], F32)
-            (nc.vector if j == TILES - 1 else nc.gpsimd).tensor_scalar(out=mean[:], in0=cube_sum[2 * j][:], scalar1=cube_sum[2 * j + 1][:], scalar2=EPS, op0=ALU.add, op1=ALU.add)
+            (nc.vector if j >= 5 else nc.gpsimd).tensor_scalar(out=mean[:], in0=cube_sum[2 * j][:], scalar1=cube_sum[2 * j + 1][:], scalar2=EPS, op0=ALU.add, op1=ALU.add)
             inv_norm = kept("inv_norm%d" % j, [P, 1], F32)
             nc.gpsimd.tensor_tensor(out=inv_norm[:], in0=mean[:], in1=expo[:], op=ALU.pow)
             inv_norms[j] = inv_norm
@@ -248,44 +250,48 @@ def tile_weightedsignedsquarepowerstep_kernel(tc, x_bytes, x_scale, a, w, d, out
             last = j >= 5
             inv_norm = inv_norms[j]
             rows = out[cols(j // 2, 2 * P), :].rearrange("(p j) k -> p j k", j=2)
-            for gk in range(PASSES):
-                res = work.tile([P, BANK], F32, name="res", tag="res", bufs=8)
-                src = square[2 * j + gk][:].rearrange("s p t -> s (p t)")
-                if not last:
-                    nc.gpsimd.tensor_scalar(out=res[:], in0=src, scalar1=inv_norm[:], scalar2=0.0, op0=ALU.mult, op1=ALU.add)
-                elif gk == 0 or j < TILES - 1:
-                    nc.scalar.activation(out=res[:], in_=src, func=ACT.Copy, scale=inv_norm[:])
-                else:
-                    nc.vector.tensor_scalar(out=res[:], in0=src, scalar1=inv_norm[:], scalar2=None, op0=ALU.mult)
-                nc.sync.dma_start(out=rows[:, j % 2, cols(gk, PASS)], in_=res[:])
+            res = work.tile([P, K], F32, name="res", tag="res", bufs=4)
+            src = squares[j][:]
+            if not last:
+                nc.gpsimd.tensor_scalar(out=res[:], in0=src, scalar1=inv_norm[:], scalar2=0.0, op0=ALU.mult, op1=ALU.add)
+                nc.sync.dma_start(out=rows[:, j % 2, :], in_=res[:])
+            else:
+                split = K if j < TILES - 1 else 384
+                if split > 0:
+                    nc.scalar.activation(out=res[:, :split], in_=src[:, :split], func=ACT.Copy, scale=inv_norm[:])
+                    nc.sync.dma_start(out=rows[:, j % 2, :split], in_=res[:, :split])
+                if split < K:
+                    nc.vector.tensor_scalar(out=res[:, split:], in0=src[:, split:], scalar1=inv_norm[:], scalar2=None, op0=ALU.mult)
+                    nc.sync.dma_start(out=rows[:, j % 2, split:], in_=res[:, split:])
 
         R = HEAD_RING
+        sign_a(0); sign_a(1)
         turn_a(0, R, 2); scale_x(0)
-        turn_a(1, R); scale_x(1); quant_a1(0); quant_a1(1)
+        turn_a(1, R); sign_a(2); sign_a(3); scale_x(1); quant_a1(0); quant_a1(1)
         turn_x(0, R, 2); scale_x(2)
-        group_a(0, 0, R); quant_x(0); scale_x(3)
-        turn_a(2, R)
+        group_a(0, 0, R); quant_x(0)
+        turn_a(2, R); sign_a(4); sign_a(5)
         turn_a(3, R); quant_a1(2)
-        turn_x(1, R); quant_a1(3); scale_x(4)
-        group_a(0, 1, R); quant_x(1); prepare_d()
-        first_stage(0); quant_a2(0, 0)
-        turn_a(4, R)
-        first_stage(2); quant_a1(4); scale_x(5)
+        group_a(0, 1, R); quant_a1(3); sign_a(6); sign_a(7)
+        turn_x(1, R); scale_x(3)
+        turn_a(4, R); quant_x(1); prepare_d()
+        first_stage(0); quant_a1(4)
+        group_a(0, 2, R); quant_a2(0, 0)
         turn_a(5, R)
-        group_a(1, 0, R); quant_a1(5)
-        turn_a(6, R); scale_x(6)
-        turn_a(7, R); quant_a1(6)
-        group_a(1, 1, R); quant_a1(7); scale_x(7)
+        first_stage(2); quant_a1(5)
+        group_a(1, 0, R)
+        turn_a(6, R); scale_x(4)
+        group_a(0, 3, R); quant_a1(6)
+        turn_a(7, R); quant_a2(0, 1)
+        group_a(1, 1, R); quant_a1(7)
         turn_x(2, R); quant_a2(1, 0)
-        group_a(0, 2, R); quant_x(2)
-        turn_x(3, R, 0, True)
-        first_stage(1); quant_x(3)
-        group_a(0, 3, R, True); quant_u(0)
-        group_a(1, 2, R); quant_a2(0, 1)
-        first_stage(3)
-        group_a(1, 3, R, False); quant_u(1); quant_a2(1, 1)
+        group_a(1, 2, R); quant_x(2)
+        first_stage(1)
+        turn_x(3, R); quant_u(0)
+        group_a(1, 3, R); quant_x(3)
+        first_stage(3); quant_a2(1, 1); quant_u(1)
         late = {0: 4, 2: 5, 4: 6, 6: 7}
-        late_scale = {}
+        late_scale = {0: 5, 1: 6, 2: 7}
         cubed = 0
         for step in range(UNITS + BACK_LAG + 1):
             ahead, back = step + LEAD, step - BACK_LAG

@@ -20,11 +20,26 @@ PACK = 4
 PASS = P * PACK
 PASSES = 2
 BANK = 512
+QUARTER = 256
 TILES = S // P
 UNITS = TILES * PASSES
 EPS = 1e-6
+
 LEAD = 4
 BACK_LAG = 2
+HEAD_TILES = 4
+TAIL_TILES = 3
+LAST_SPLIT = 384
+PAIR = 2
+
+Y_BANKS = (0, 1)
+T_BANKS = (2, 3)
+Z_BANKS = (4, 5, 6, 7)
+HEAD_BANKS = (3, 4, 5, 6, 7, 2)
+
+
+def cols(i, width=P):
+    return slice(i * width, (i + 1) * width)
 
 
 def tile_weightedsignedsquarepowerstep_kernel(tc, x_bytes, x_scale, a, w, d, out):
@@ -33,27 +48,19 @@ def tile_weightedsignedsquarepowerstep_kernel(tc, x_bytes, x_scale, a, w, d, out
         keep = ctx.enter_context(tc.tile_pool(name="keep", bufs=1))
         work = ctx.enter_context(tc.tile_pool(name="work", bufs=3))
         psum = ctx.enter_context(tc.psum_pool(name="psum", bufs=1))
-        ctx.enter_context(nc.allow_non_contiguous_dma(reason="small vectors in runs of four"))
+        ctx.enter_context(nc.allow_non_contiguous_dma(reason="x_scale, w and d are spread over the partitions"))
         ctx.enter_context(tc.manual_schedule())
 
         def kept(name, shape, dtype):
             return keep.tile(shape, dtype, name=name, align_bytes=64)
 
-        turns = {}
+        uses = {}
 
-        def bank(ring, dtype=F32):
-            n = turns.get(ring, 0)
-            turns[ring] = n + 1
+        def next_bank(banks, dtype=F32):
+            n = uses.get(banks, 0)
+            uses[banks] = n + 1
             width = BANK if dtype == F32 else 2 * BANK
-            return psum.tile([P, width], dtype, name="bank", tag="bank%d" % ring[n % len(ring)])
-
-        HEAD_RING = (3, 4, 5, 6, 7, 2)
-        Y_RING = (0, 1)
-        T_RING = (2, 3)
-        Z_RING = (4, 5, 6, 7)
-
-        def cols(i, width=P):
-            return slice(i * width, (i + 1) * width)
+            return psum.tile([P, width], dtype, name="bank", tag="bank%d" % banks[n % len(banks)])
 
         xs_col = kept("xs_col", [P, PASSES, PACK], F32)
         w_col = kept("w_col", [P, PASSES, PACK], BF16)
@@ -66,11 +73,16 @@ def tile_weightedsignedsquarepowerstep_kernel(tc, x_bytes, x_scale, a, w, d, out
 
         def load_a(g, h):
             rows = a[cols(g, PASS), :].rearrange("(p t) k -> p t k", t=PACK)
-            nc.sync.dma_start(out=a_rows[g][h][:], in_=rows[:, 2 * h : 2 * h + 2, :])
+            nc.sync.dma_start(out=a_rows[g][h][:], in_=rows[:, cols(h, 2), :])
 
         nc.sync.dma_start(out=xs_col[:], in_=x_scale.rearrange("o (g p t) -> p (o g) t", g=PASSES, t=PACK))
         nc.sync.dma_start(out=w_col[:], in_=w.rearrange("(g p t) -> p g t", g=PASSES, t=PACK))
-        load_a(0, 0); load_x(0); load_a(0, 1); load_x(1); load_a(1, 0); load_a(1, 1)
+        load_a(0, 0)
+        load_x(0)
+        load_a(0, 1)
+        load_x(1)
+        load_a(1, 0)
+        load_a(1, 1)
         load_x(2)
         load_x(3)
         nc.sync.dma_start(out=d_col[:, :, 0], in_=d.rearrange("(j p) -> p j", p=P))
@@ -82,39 +94,40 @@ def tile_weightedsignedsquarepowerstep_kernel(tc, x_bytes, x_scale, a, w, d, out
         make_identity(nc, ident[:])
         one = kept("one", [P, 1], F32)
         nc.gpsimd.memset(one[:], 1.0)
-        expo = kept("expo", [P, 1], F32)
-        nc.gpsimd.tensor_scalar(out=expo[:], in0=one[:], scalar1=-2.0 / 3.0, scalar2=0.0, op0=ALU.mult, op1=ALU.add)
-        warm = kept("warm", [P, 1], F32)
-        nc.scalar.activation(out=warm[:], in_=one[:], func=ACT.Abs)
+        exponent = kept("exponent", [P, 1], F32)
+        nc.gpsimd.tensor_scalar(out=exponent[:], in0=one[:], scalar1=-2.0 / 3.0, scalar2=0.0, op0=ALU.mult, op1=ALU.add)
+        eps = kept("eps", [P, 1], F32)
+        nc.scalar.activation(out=eps[:], in_=one[:], func=ACT.Abs, scale=EPS)
 
-        def warm_up(b, count):
+        def warm_up(bank, count):
             for i in range(count):
-                nc.tensor.matmul(b[:, cols(i)], lhsT=ident[:], rhs=ident[:], start=True, stop=True)
+                nc.tensor.matmul(bank[:, cols(i)], lhsT=ident[:], rhs=ident[:], start=True, stop=True)
 
+        w_flat = w_col[:].rearrange("p g t -> p (g t)")
         w_f32 = kept("w_f32", [P, PASSES * PACK], F32)
-        d_f32 = kept("d_f32", [P, PASSES * PACK], F32)
         half_sign = kept("half_sign", [P, PASSES * PACK], F32)
-        ident_bf = kept("ident_bf", [P, P], BF16)
-        nc.vector.tensor_copy(out=ident_bf[:], in_=ident[:])
-        nc.vector.tensor_copy(out=w_f32[:], in_=w_col[:].rearrange("p g t -> p (g t)"))
-        nc.vector.tensor_scalar(out=half_sign[:], in0=w_col[:].rearrange("p g t -> p (g t)"), scalar1=0.0, scalar2=-0.5, op0=ALU.is_ge, op1=ALU.add)
-        signed = [kept("signed%d" % g, [P, PACK, K], BF16) for g in range(PASSES)]
-
-        def sign_a(i):
-            nc.vector.tensor_scalar(out=signed[i // PACK][:, i % PACK, :], in0=a_slot(i // PACK, i % PACK), scalar1=half_sign[:, i : i + 1], scalar2=2.0, op0=ALU.mult, op1=ALU.mult)
+        signs = kept("signs", [P, PASSES * PACK, P], BF16)
+        nc.vector.tensor_copy(out=w_f32[:], in_=w_flat)
+        nc.vector.tensor_scalar(out=half_sign[:], in0=w_flat, scalar1=0.0, scalar2=-0.5, op0=ALU.is_ge, op1=ALU.add)
+        for i in range(PASSES * PACK):
+            nc.vector.tensor_scalar(
+                out=signs[:, i, :], in0=ident[:], scalar1=half_sign[:, i : i + 1], scalar2=2.0, op0=ALU.mult, op1=ALU.mult
+            )
 
         xs_all = kept("xs_all", [P, K], F32)
         for g in range(PASSES):
-            b = bank(HEAD_RING)
-            warm_up(b, 3 if g == 0 else 0)
+            bank = next_bank(HEAD_BANKS)
+            warm_up(bank, 3 if g == 0 else 0)
             for t in range(PACK):
-                nc.tensor.transpose(b[:, cols(t)], xs_col[:, g, t : t + 1].to_broadcast([P, P]), ident[:])
-            (nc.vector.tensor_copy if g == 9 else nc.scalar.copy)(
+                nc.tensor.transpose(bank[:, cols(t)], xs_col[:, g, t : t + 1].to_broadcast([P, P]), ident[:])
+            nc.scalar.copy(
                 out=xs_all[:, cols(g, PASS)].rearrange("c (p t) -> c p t", t=PACK),
-                in_=b[:].rearrange("c (t p) -> c p t", t=PACK),
+                in_=bank[:].rearrange("c (t p) -> c p t", t=PACK),
             )
 
-        def prepare_d():
+        d_f32 = kept("d_f32", [P, K // P], F32)
+
+        def widen_d():
             nc.vector.tensor_copy(out=d_f32[:], in_=d_col[:, :, 0])
 
         def quantize(name, grouped, words):
@@ -123,198 +136,190 @@ def tile_weightedsignedsquarepowerstep_kernel(tc, x_bytes, x_scale, a, w, d, out
             nc.vector.quantize_mx(out=codes[:].bitcast(FP8X4), scales=scales[:], in_=grouped)
             return codes, scales
 
-        def mx(dst, lhs, lhs_cols, rhs, rhs_cols, g):
+        def mx_pass(dst, lhs, lhs_cols, rhs, g):
             nc.tensor.matmul_mx(
                 out=dst,
                 lhsT=lhs[0][:, lhs_cols].bitcast(FP8X4),
                 lhsT_scale=lhs[1][:, lhs_cols],
-                rhs=rhs[0][:, rhs_cols].bitcast(FP8X4),
-                rhs_scale=rhs[1][:, rhs_cols],
+                rhs=rhs[0][:, cols(g)].bitcast(FP8X4),
+                rhs_scale=rhs[1][:, cols(g)],
                 start=(g == 0),
                 stop=(g == PASSES - 1),
             )
 
-        turned = {}
-
-        def turn(key, rows, ring, warm_count, on_vector):
+        def turn(rows, banks, warm_count, on_vector):
             words = rows.bitcast(F32)
-            b = bank(ring)
-            warm_up(b, warm_count)
+            bank = next_bank(banks)
+            warm_up(bank, warm_count)
             for g in range(PASSES):
-                for u in range(2):
-                    nc.tensor.transpose(b[:, cols(2 * g + u)], words[:, 256 * g + u : 256 * (g + 1) : 2], ident[:])
+                for e in range(2):
+                    nc.tensor.transpose(bank[:, cols(2 * g + e)], words[:, 256 * g + e : 256 * (g + 1) : 2], ident[:])
             grouped = work.tile([P, K], BF16, name="grouped", tag="grouped", bufs=4, align_bytes=64)
             (nc.vector.tensor_copy if on_vector else nc.scalar.copy)(
-                out=grouped[:].bitcast(F32).rearrange("p (g r u) -> p g r u", g=PASSES, u=2),
-                in_=b[:].rearrange("p (g u r) -> p g r u", g=PASSES, u=2),
+                out=grouped[:].bitcast(F32).rearrange("p (g r e) -> p g r e", g=PASSES, e=2),
+                in_=bank[:].rearrange("p (g e r) -> p g r e", g=PASSES, e=2),
             )
-            turned[key] = grouped
+            return grouped
 
-        x_scaled = {}
-        xq, aq1, aq2, uq = {}, {}, {}, {}
+        x_scaled, x_turned, a_turned, a_grouped, u_grouped = {}, {}, {}, {}, {}
+        xq, aq_k, aq_m, uq = {}, {}, {}, {}
 
         def scale_x(j):
             x_scaled[j] = kept("x_scaled%d" % j, [P, K], BF16)
             nc.vector.tensor_tensor(out=x_scaled[j][:], in0=xbytes[j // 2][:, j % 2, :].bitcast(FP8), in1=xs_all[:], op=ALU.mult)
 
-        def turn_x(j, ring, warm_count=0, on_vector=False):
-            turn(("x", j), x_scaled[j][:], ring, warm_count, on_vector)
+        def turn_x(j, banks=HEAD_BANKS, warm_count=0, on_vector=False):
+            x_turned[j] = turn(x_scaled[j][:], banks, warm_count, on_vector)
 
-        def quant_x(j):
-            xq[j] = quantize("xq%d" % j, turned[("x", j)][:], K // PACK)
+        def quantize_x(j):
+            xq[j] = quantize("xq%d" % j, x_turned[j][:], K // PACK)
 
-        def turn_a(i, ring, warm_count=0, on_vector=False):
-            turn(("a", i), a_slot(i // PACK, i % PACK), ring, warm_count, on_vector)
+        def turn_a(i, warm_count=0):
+            a_turned[i] = turn(a_slot(i // PACK, i % PACK), HEAD_BANKS, warm_count, False)
 
-        def quant_a1(i):
-            aq1[i] = quantize("aq1_%d" % i, turned[("a", i)][:], K // PACK)
+        def quantize_a_k(i):
+            aq_k[i] = quantize("aq_k%d" % i, a_turned[i][:], K // PACK)
 
-        a_grouped = {}
-
-        def group_a(gm, q, ring, on_vector=False):
+        def group_a(gm, q, on_vector=False):
             gk, h = q // 2, q % 2
-            b = bank(ring, BF16)
-            for e in range(2):
-                nc.tensor.matmul(b[:, cols(e, PASS)], lhsT=ident_bf[:], rhs=signed[gm][:, :, cols(2 * q + e)].rearrange("p t k -> p k t"), start=True, stop=True)
+            bank = next_bank(HEAD_BANKS, BF16)
+            for t in range(PACK):
+                nc.tensor.matmul(
+                    bank[:, cols(t, QUARTER)], lhsT=signs[:, gm * PACK + t, :], rhs=a_slot(gm, t)[:, cols(q, QUARTER)],
+                    start=True, stop=True,
+                )
             if h == 0:
-                a_grouped[gm, gk] = kept("a_grouped%d%d" % (gm, gk), [P, PASS * PACK], BF16)
-            nc.scalar.copy(out=a_grouped[gm, gk][:, cols(h, 2 * PASS)], in_=b[:])
+                a_grouped[gm, gk] = kept("a_grouped%d%d" % (gm, gk), [P, PASS, PACK], BF16)
+            (nc.vector.tensor_copy if on_vector else nc.scalar.copy)(
+                out=a_grouped[gm, gk][:, cols(h, QUARTER), :], in_=bank[:].rearrange("p (t k) -> p k t", t=PACK)
+            )
 
-        def quant_a2(gm, gk):
-            aq2[gm, gk] = quantize("aq2_%d%d" % (gm, gk), a_grouped[gm, gk][:], PASS)
+        def quantize_a_m(gm, gk):
+            aq_m[gm, gk] = quantize("aq_m%d%d" % (gm, gk), a_grouped[gm, gk][:].rearrange("p k t -> p (k t)"), PASS)
 
-        u_grouped = {}
-
-        def first_stage(n):
+        def first_product(n):
             j, gm = n // PASSES, n % PASSES
-            b = bank(Y_RING)
+            bank = next_bank(Y_BANKS)
             for t in range(PACK):
                 for g in range(PASSES):
-                    mx(b[:, cols(t)], aq1[gm * PACK + t], cols(g), xq[j], cols(g), g)
-            wy = work.tile([P, BANK], F32, name="wy", tag="wy")
+                    mx_pass(bank[:, cols(t)], aq_k[gm * PACK + t], cols(g), xq[j], g)
+            abs_wy = work.tile([P, BANK], F32, name="abs_wy", tag="abs_wy")
             for t in range(PACK):
-                nc.scalar.activation(out=wy[:, cols(t)], in_=b[:, cols(t)], func=ACT.Abs, scale=w_f32[:, gm * PACK + t : gm * PACK + t + 1])
+                i = gm * PACK + t
+                nc.scalar.activation(out=abs_wy[:, cols(t)], in_=bank[:, cols(t)], func=ACT.Abs, scale=w_f32[:, i : i + 1])
             if gm == 0:
                 u_grouped[j] = kept("u_grouped%d" % j, [P, M], BF16)
             nc.vector.tensor_tensor(
-                out=u_grouped[j][:, cols(gm, PASS)].rearrange("p (r i t) -> p r t i", i=4, t=PACK),
-                in0=b[:].rearrange("p (t r i) -> p r t i", t=PACK, i=4),
-                in1=wy[:].rearrange("p (t r i) -> p r t i", t=PACK, i=4),
+                out=u_grouped[j][:, cols(gm, PASS)].rearrange("p (r i t) -> p r t i", i=PAIR, t=PACK),
+                in0=bank[:].rearrange("p (t r i) -> p r t i", t=PACK, i=PAIR),
+                in1=abs_wy[:].rearrange("p (t r i) -> p r t i", t=PACK, i=PAIR),
                 op=ALU.mult,
             )
 
-        def quant_u(j):
+        def quantize_u(j):
             uq[j] = quantize("uq%d" % j, u_grouped[j][:], M // PACK)
 
-        z_cols = {}
+        z_cols, z_rows, squares, cube_sums, inv_norms = {}, {}, {}, {}, {}
 
-        def second_stage(n):
+        def second_product(n):
             j, gk = n // PASSES, n % PASSES
-            b = bank(T_RING)
-            for t in range(PACK):
+            bank = next_bank(T_BANKS)
+            for i in range(PACK):
                 for g in range(PASSES):
-                    mx(b[:, cols(t)], aq2[g, gk], cols(t), uq[j], cols(g), g)
-            z_cols[n] = work.tile([P, BANK], F32, name="z", tag="z", bufs=4)
-            for t in range(PACK):
-                nc.scalar.activation(out=z_cols[n][:, cols(t)], in_=b[:, cols(t)], func=ACT.Copy, scale=d_f32[:, gk * PACK + t : gk * PACK + t + 1])
-
-        z_rows, square, squares, cube_sum = {}, {}, {}, {}
+                    mx_pass(bank[:, cols(i)], aq_m[g, gk], cols(i), uq[j], g)
+            z_cols[n] = work.tile([P, BANK], F32, name="z_cols", tag="z_cols", bufs=4)
+            for i in range(PACK):
+                block = gk * PACK + i
+                nc.scalar.activation(out=z_cols[n][:, cols(i)], in_=bank[:, cols(i)], func=ACT.Copy, scale=d_f32[:, block : block + 1])
 
         def signed_square(n):
-            b = bank(Z_RING)
-            for t in range(PACK):
-                nc.tensor.transpose(b[:, cols(t)], z_cols[n][:, cols(t)], ident[:])
-            z_rows[n] = b[:]
-            az = work.tile([P, BANK], F32, name="az", tag="az")
-            nc.scalar.activation(out=az[:], in_=z_rows[n], func=ACT.Abs)
-            if n % 2 == 0:
-                squares[n // 2] = work.tile([P, K], F32, name="sq", tag="sq", bufs=4)
-            square[n] = squares[n // 2][:, cols(n % 2, PASS)]
-            nc.vector.tensor_tensor(out=square[n], in0=z_rows[n], in1=az[:], op=ALU.mult)
+            j, gk = n // PASSES, n % PASSES
+            z_rows[n] = next_bank(Z_BANKS)
+            for i in range(PACK):
+                nc.tensor.transpose(z_rows[n][:, cols(i)], z_cols[n][:, cols(i)], ident[:])
+            abs_z = work.tile([P, BANK], F32, name="abs_z", tag="abs_z")
+            nc.scalar.activation(out=abs_z[:], in_=z_rows[n][:], func=ACT.Abs)
+            if gk == 0:
+                squares[j] = work.tile([P, K], F32, name="squares", tag="squares", bufs=4)
+            nc.vector.tensor_tensor(out=squares[j][:, cols(gk, PASS)], in0=z_rows[n][:], in1=abs_z[:], op=ALU.mult)
 
-        def cube(n):
-            cu = work.tile([P, BANK], F32, name="cu", tag="cu", bufs=2)
-            cube_sum[n] = kept("cube_sum%d" % n, [P, 1], F32)
-            nc.vector.scalar_tensor_tensor(out=cu[:], in0=z_rows[n], scalar=1.0 / K, in1=square[n], op0=ALU.mult, op1=ALU.mult, accum_out=cube_sum[n][:])
-
-        inv_norms = {}
+        def sum_cubes(n):
+            j, gk = n // PASSES, n % PASSES
+            cubes = work.tile([P, BANK], F32, name="cubes", tag="cubes", bufs=2)
+            cube_sums[n] = kept("cube_sum%d" % n, [P, 1], F32)
+            nc.vector.scalar_tensor_tensor(
+                out=cubes[:], in0=z_rows[n][:], scalar=1.0 / K, in1=squares[j][:, cols(gk, PASS)],
+                op0=ALU.mult, op1=ALU.mult, accum_out=cube_sums[n][:],
+            )
 
         def norm(j):
             mean = kept("mean%d" % j, [P, 1], F32)
-            (nc.vector if j >= 5 else nc.gpsimd).tensor_scalar(out=mean[:], in0=cube_sum[2 * j][:], scalar1=cube_sum[2 * j + 1][:], scalar2=EPS, op0=ALU.add, op1=ALU.add)
-            inv_norm = kept("inv_norm%d" % j, [P, 1], F32)
-            nc.gpsimd.tensor_tensor(out=inv_norm[:], in0=mean[:], in1=expo[:], op=ALU.pow)
-            inv_norms[j] = inv_norm
+            (nc.gpsimd if j < TILES - TAIL_TILES else nc.vector).tensor_scalar(
+                out=mean[:], in0=cube_sums[2 * j][:], scalar1=cube_sums[2 * j + 1][:], scalar2=eps[:], op0=ALU.add, op1=ALU.add
+            )
+            inv_norms[j] = kept("inv_norm%d" % j, [P, 1], F32)
+            nc.gpsimd.tensor_tensor(out=inv_norms[j][:], in0=mean[:], in1=exponent[:], op=ALU.pow)
 
-        def finish(j):
-            last = j >= 5
-            inv_norm = inv_norms[j]
-            rows = out[cols(j // 2, 2 * P), :].rearrange("(p j) k -> p j k", j=2)
+        def scale_and_store(j):
+            rows = out[cols(j // 2, 2 * P), :].rearrange("(p j) k -> p j k", j=2)[:, j % 2, :]
             res = work.tile([P, K], F32, name="res", tag="res", bufs=4)
-            src = squares[j][:]
-            if not last:
-                nc.gpsimd.tensor_scalar(out=res[:], in0=src, scalar1=inv_norm[:], scalar2=0.0, op0=ALU.mult, op1=ALU.add)
-                nc.sync.dma_start(out=rows[:, j % 2, :], in_=res[:])
+            if j < TILES - TAIL_TILES:
+                nc.gpsimd.tensor_scalar(out=res[:], in0=squares[j][:], scalar1=inv_norms[j][:], scalar2=0.0, op0=ALU.mult, op1=ALU.add)
+                nc.sync.dma_start(out=rows, in_=res[:])
             else:
-                split = K if j < TILES - 1 else 384
-                if split > 0:
-                    nc.scalar.activation(out=res[:, :split], in_=src[:, :split], func=ACT.Copy, scale=inv_norm[:])
-                    nc.sync.dma_start(out=rows[:, j % 2, :split], in_=res[:, :split])
+                split = K if j < TILES - 1 else LAST_SPLIT
+                nc.scalar.activation(out=res[:, :split], in_=squares[j][:, :split], func=ACT.Copy, scale=inv_norms[j][:])
+                nc.sync.dma_start(out=rows[:, :split], in_=res[:, :split])
                 if split < K:
-                    nc.vector.tensor_scalar(out=res[:, split:], in0=src[:, split:], scalar1=inv_norm[:], scalar2=None, op0=ALU.mult)
-                    nc.sync.dma_start(out=rows[:, j % 2, split:], in_=res[:, split:])
+                    nc.vector.tensor_scalar(out=res[:, split:], in0=squares[j][:, split:], scalar1=inv_norms[j][:], scalar2=None, op0=ALU.mult)
+                    nc.sync.dma_start(out=rows[:, split:], in_=res[:, split:])
 
-        R = HEAD_RING
-        sign_a(0); sign_a(1)
-        turn_a(0, R, 2); scale_x(0)
-        turn_a(1, R); sign_a(2); sign_a(3); scale_x(1); quant_a1(0); quant_a1(1)
-        turn_x(0, R, 2); scale_x(2)
-        group_a(0, 0, R); quant_x(0)
-        turn_a(2, R); sign_a(4); sign_a(5)
-        turn_a(3, R); quant_a1(2)
-        group_a(0, 1, R); quant_a1(3); sign_a(6); sign_a(7)
-        turn_x(1, R); scale_x(3)
-        turn_a(4, R); quant_x(1); prepare_d()
-        first_stage(0); quant_a1(4)
-        group_a(0, 2, R); quant_a2(0, 0)
-        turn_a(5, R)
-        first_stage(2); quant_a1(5)
-        group_a(1, 0, R)
-        turn_a(6, R); scale_x(4)
-        group_a(0, 3, R); quant_a1(6)
-        turn_a(7, R); quant_a2(0, 1)
-        group_a(1, 1, R); quant_a1(7)
-        turn_x(2, R); quant_a2(1, 0)
-        group_a(1, 2, R); quant_x(2)
-        first_stage(1)
-        turn_x(3, R); quant_u(0)
-        group_a(1, 3, R); quant_x(3)
-        first_stage(3); quant_a2(1, 1); quant_u(1)
-        late = {0: 4, 2: 5, 4: 6, 6: 7}
-        late_scale = {0: 5, 1: 6, 2: 7}
-        cubed = 0
+        turn_a(0, warm_count=2); scale_x(0)
+        turn_a(1); scale_x(1); quantize_a_k(0); quantize_a_k(1)
+        turn_x(0, warm_count=2); scale_x(2)
+        group_a(0, 0); quantize_x(0); scale_x(3)
+        turn_a(2)
+        turn_a(3); quantize_a_k(2)
+        turn_x(1); quantize_a_k(3); scale_x(4)
+        group_a(0, 1); quantize_x(1); widen_d()
+        first_product(0); quantize_a_m(0, 0)
+        turn_a(4)
+        first_product(2); quantize_a_k(4); scale_x(5)
+        turn_a(5)
+        group_a(1, 0); quantize_a_k(5)
+        turn_a(6); scale_x(6)
+        turn_a(7); quantize_a_k(6)
+        group_a(1, 1); quantize_a_k(7); scale_x(7)
+        turn_x(2); quantize_a_m(1, 0)
+        group_a(0, 2); quantize_x(2)
+        turn_x(3, on_vector=True)
+        first_product(1); quantize_x(3)
+        group_a(0, 3, on_vector=True); quantize_u(0)
+        group_a(1, 2); quantize_a_m(0, 1)
+        first_product(3)
+        group_a(1, 3); quantize_u(1); quantize_a_m(1, 1)
+
         for step in range(UNITS + BACK_LAG + 1):
             ahead, back = step + LEAD, step - BACK_LAG
+            late_tile = HEAD_TILES + step // 2
             if 0 <= back < UNITS:
                 signed_square(back)
             if ahead < UNITS:
-                first_stage(ahead)
-            if step - 1 in late:
-                quant_x(late[step - 1])
-            if cubed < back + (1 if ahead < UNITS else 0):
-                cube(cubed)
-                cubed = cubed + 1
-                if cubed % 2 == 0:
-                    norm(cubed // 2 - 1)
-                    if cubed // 2 <= 5:
-                        finish(cubed // 2 - 1)
+                first_product(ahead)
+            if step % 2 == 1 and late_tile < TILES:
+                quantize_x(late_tile)
+            cubed = back if ahead < UNITS else back - 1
+            if cubed >= 0 and ahead != UNITS:
+                sum_cubes(cubed)
+                if cubed % 2 == 1:
+                    norm(cubed // 2)
+                    if cubed // 2 < TILES - TAIL_TILES:
+                        scale_and_store(cubed // 2)
             if ahead % 2 == 1 and ahead < UNITS:
-                quant_u(ahead // 2)
-            if step in late_scale:
-                scale_x(late_scale[step])
+                quantize_u(ahead // 2)
             if step < UNITS:
-                second_stage(step)
-            if step in late:
-                turn_x(late[step], Z_RING)
-        for j in range(5, TILES):
-            finish(j)
+                second_product(step)
+            if step % 2 == 0 and late_tile < TILES:
+                turn_x(late_tile, Z_BANKS)
+        for j in range(TILES - TAIL_TILES, TILES):
+            scale_and_store(j)

from contextlib import ExitStack

import concourse.mybir as mybir
from concourse.masks import make_identity

S, K, M = 1024, 1024, 1024
FLOPS = 2 * 2 * S * K * M

F32 = mybir.dt.float32
BF16 = mybir.dt.bfloat16
U32 = mybir.dt.uint32
U8 = mybir.dt.uint8
FP8 = mybir.dt.float8_e4m3fn
FP8X4 = mybir.dt.float8_e4m3fn_x4
ALU = mybir.AluOpType
ACT = mybir.ActivationFunctionType

P = 128
PACK = 4
PASS = P * PACK
PASSES = 2
BANK = 512
QUARTER = 256
TILES = S // P
UNITS = TILES * PASSES
EPS = 1e-6

LEAD = 4
BACK_LAG = 2
HEAD_TILES = 4
TAIL_TILES = 3
LAST_SPLIT = 384
PAIR = 2

Y_BANKS = (0, 1)
T_BANKS = (2, 3)
Z_BANKS = (4, 5, 6, 7)
HEAD_BANKS = (3, 4, 5, 6, 7, 2)


def cols(i, width=P):
    return slice(i * width, (i + 1) * width)


def tile_weightedsignedsquarepowerstep_kernel(tc, x_bytes, x_scale, a, w, d, out):
    nc = tc.nc
    with ExitStack() as ctx:
        keep = ctx.enter_context(tc.tile_pool(name="keep", bufs=1))
        work = ctx.enter_context(tc.tile_pool(name="work", bufs=3))
        psum = ctx.enter_context(tc.psum_pool(name="psum", bufs=1))
        ctx.enter_context(nc.allow_non_contiguous_dma(reason="x_scale, w and d are spread over the partitions"))
        ctx.enter_context(tc.manual_schedule())

        def kept(name, shape, dtype):
            return keep.tile(shape, dtype, name=name, align_bytes=64)

        uses = {}

        def next_bank(banks, dtype=F32):
            n = uses.get(banks, 0)
            uses[banks] = n + 1
            width = BANK if dtype == F32 else 2 * BANK
            return psum.tile([P, width], dtype, name="bank", tag="bank%d" % banks[n % len(banks)])

        xs_col = kept("xs_col", [P, PASSES, PACK], F32)
        w_col = kept("w_col", [P, PASSES, PACK], BF16)
        d_col = kept("d_col", [P, K // P, 2], BF16)
        xbytes = [kept("xbytes%d" % c, [P, 2, K], U8) for c in range(TILES // 2)]
        a_rows = [[kept("a_rows%d%d" % (g, h), [P, 2, K], BF16) for h in range(2)] for g in range(PASSES)]

        def load_x(c):
            nc.sync.dma_start(out=xbytes[c][:], in_=x_bytes[cols(c, 2 * P), :].rearrange("(p j) k -> p j k", j=2))

        def load_a(g, h):
            rows = a[cols(g, PASS), :].rearrange("(p t) k -> p t k", t=PACK)
            nc.sync.dma_start(out=a_rows[g][h][:], in_=rows[:, cols(h, 2), :])

        nc.sync.dma_start(out=xs_col[:], in_=x_scale.rearrange("o (g p t) -> p (o g) t", g=PASSES, t=PACK))
        nc.sync.dma_start(out=w_col[:], in_=w.rearrange("(g p t) -> p g t", g=PASSES, t=PACK))
        load_a(0, 0)
        load_x(0)
        load_a(0, 1)
        load_x(1)
        load_a(1, 0)
        load_a(1, 1)
        load_x(2)
        load_x(3)
        nc.sync.dma_start(out=d_col[:, :, 0], in_=d.rearrange("(j p) -> p j", p=P))

        def a_slot(g, t):
            return a_rows[g][t // 2][:, t % 2, :]

        ident = kept("ident", [P, P], F32)
        make_identity(nc, ident[:])
        one = kept("one", [P, 1], F32)
        nc.gpsimd.memset(one[:], 1.0)
        exponent = kept("exponent", [P, 1], F32)
        nc.gpsimd.tensor_scalar(out=exponent[:], in0=one[:], scalar1=-2.0 / 3.0, scalar2=0.0, op0=ALU.mult, op1=ALU.add)
        eps = kept("eps", [P, 1], F32)
        nc.scalar.activation(out=eps[:], in_=one[:], func=ACT.Abs, scale=EPS)

        def warm_up(bank, count):
            for i in range(count):
                nc.tensor.matmul(bank[:, cols(i)], lhsT=ident[:], rhs=ident[:], start=True, stop=True)

        w_flat = w_col[:].rearrange("p g t -> p (g t)")
        w_f32 = kept("w_f32", [P, PASSES * PACK], F32)
        half_sign = kept("half_sign", [P, PASSES * PACK], F32)
        signs = kept("signs", [P, PASSES * PACK, P], BF16)
        nc.vector.tensor_copy(out=w_f32[:], in_=w_flat)
        nc.vector.tensor_scalar(out=half_sign[:], in0=w_flat, scalar1=0.0, scalar2=-0.5, op0=ALU.is_ge, op1=ALU.add)
        for i in range(PASSES * PACK):
            nc.vector.tensor_scalar(
                out=signs[:, i, :], in0=ident[:], scalar1=half_sign[:, i : i + 1], scalar2=2.0, op0=ALU.mult, op1=ALU.mult
            )

        xs_all = kept("xs_all", [P, K], F32)
        for g in range(PASSES):
            bank = next_bank(HEAD_BANKS)
            warm_up(bank, 3 if g == 0 else 0)
            for t in range(PACK):
                nc.tensor.transpose(bank[:, cols(t)], xs_col[:, g, t : t + 1].to_broadcast([P, P]), ident[:])
            nc.scalar.copy(
                out=xs_all[:, cols(g, PASS)].rearrange("c (p t) -> c p t", t=PACK),
                in_=bank[:].rearrange("c (t p) -> c p t", t=PACK),
            )

        d_f32 = kept("d_f32", [P, K // P], F32)

        def widen_d():
            nc.vector.tensor_copy(out=d_f32[:], in_=d_col[:, :, 0])

        def quantize(name, grouped, words):
            codes = kept(name + "_codes", [P, words], U32)
            scales = kept(name + "_scales", [P, words], U8)
            nc.vector.quantize_mx(out=codes[:].bitcast(FP8X4), scales=scales[:], in_=grouped)
            return codes, scales

        def mx_pass(dst, lhs, lhs_cols, rhs, g):
            nc.tensor.matmul_mx(
                out=dst,
                lhsT=lhs[0][:, lhs_cols].bitcast(FP8X4),
                lhsT_scale=lhs[1][:, lhs_cols],
                rhs=rhs[0][:, cols(g)].bitcast(FP8X4),
                rhs_scale=rhs[1][:, cols(g)],
                start=(g == 0),
                stop=(g == PASSES - 1),
            )

        def turn(rows, banks, warm_count, on_vector):
            words = rows.bitcast(F32)
            bank = next_bank(banks)
            warm_up(bank, warm_count)
            for g in range(PASSES):
                for e in range(2):
                    nc.tensor.transpose(bank[:, cols(2 * g + e)], words[:, 256 * g + e : 256 * (g + 1) : 2], ident[:])
            grouped = work.tile([P, K], BF16, name="grouped", tag="grouped", bufs=4, align_bytes=64)
            (nc.vector.tensor_copy if on_vector else nc.scalar.copy)(
                out=grouped[:].bitcast(F32).rearrange("p (g r e) -> p g r e", g=PASSES, e=2),
                in_=bank[:].rearrange("p (g e r) -> p g r e", g=PASSES, e=2),
            )
            return grouped

        x_scaled, x_turned, a_turned, a_grouped, u_grouped = {}, {}, {}, {}, {}
        xq, aq_k, aq_m, uq = {}, {}, {}, {}

        def scale_x(j):
            x_scaled[j] = kept("x_scaled%d" % j, [P, K], BF16)
            nc.vector.tensor_tensor(out=x_scaled[j][:], in0=xbytes[j // 2][:, j % 2, :].bitcast(FP8), in1=xs_all[:], op=ALU.mult)

        def turn_x(j, banks=HEAD_BANKS, warm_count=0, on_vector=False):
            x_turned[j] = turn(x_scaled[j][:], banks, warm_count, on_vector)

        def quantize_x(j):
            xq[j] = quantize("xq%d" % j, x_turned[j][:], K // PACK)

        def turn_a(i, warm_count=0):
            a_turned[i] = turn(a_slot(i // PACK, i % PACK), HEAD_BANKS, warm_count, False)

        def quantize_a_k(i):
            aq_k[i] = quantize("aq_k%d" % i, a_turned[i][:], K // PACK)

        def group_a(gm, q, on_vector=False):
            gk, h = q // 2, q % 2
            bank = next_bank(HEAD_BANKS, BF16)
            for t in range(PACK):
                nc.tensor.matmul(
                    bank[:, cols(t, QUARTER)], lhsT=signs[:, gm * PACK + t, :], rhs=a_slot(gm, t)[:, cols(q, QUARTER)],
                    start=True, stop=True,
                )
            if h == 0:
                a_grouped[gm, gk] = kept("a_grouped%d%d" % (gm, gk), [P, PASS, PACK], BF16)
            (nc.vector.tensor_copy if on_vector else nc.scalar.copy)(
                out=a_grouped[gm, gk][:, cols(h, QUARTER), :], in_=bank[:].rearrange("p (t k) -> p k t", t=PACK)
            )

        def quantize_a_m(gm, gk):
            aq_m[gm, gk] = quantize("aq_m%d%d" % (gm, gk), a_grouped[gm, gk][:].rearrange("p k t -> p (k t)"), PASS)

        def first_product(n):
            j, gm = n // PASSES, n % PASSES
            bank = next_bank(Y_BANKS)
            for t in range(PACK):
                for g in range(PASSES):
                    mx_pass(bank[:, cols(t)], aq_k[gm * PACK + t], cols(g), xq[j], g)
            abs_wy = work.tile([P, BANK], F32, name="abs_wy", tag="abs_wy")
            for t in range(PACK):
                i = gm * PACK + t
                nc.scalar.activation(out=abs_wy[:, cols(t)], in_=bank[:, cols(t)], func=ACT.Abs, scale=w_f32[:, i : i + 1])
            if gm == 0:
                u_grouped[j] = kept("u_grouped%d" % j, [P, M], BF16)
            nc.vector.tensor_tensor(
                out=u_grouped[j][:, cols(gm, PASS)].rearrange("p (r i t) -> p r t i", i=PAIR, t=PACK),
                in0=bank[:].rearrange("p (t r i) -> p r t i", t=PACK, i=PAIR),
                in1=abs_wy[:].rearrange("p (t r i) -> p r t i", t=PACK, i=PAIR),
                op=ALU.mult,
            )

        def quantize_u(j):
            uq[j] = quantize("uq%d" % j, u_grouped[j][:], M // PACK)

        z_cols, z_rows, squares, cube_sums, inv_norms = {}, {}, {}, {}, {}

        def second_product(n):
            j, gk = n // PASSES, n % PASSES
            bank = next_bank(T_BANKS)
            for i in range(PACK):
                for g in range(PASSES):
                    mx_pass(bank[:, cols(i)], aq_m[g, gk], cols(i), uq[j], g)
            z_cols[n] = work.tile([P, BANK], F32, name="z_cols", tag="z_cols", bufs=4)
            for i in range(PACK):
                block = gk * PACK + i
                nc.scalar.activation(out=z_cols[n][:, cols(i)], in_=bank[:, cols(i)], func=ACT.Copy, scale=d_f32[:, block : block + 1])

        def signed_square(n):
            j, gk = n // PASSES, n % PASSES
            z_rows[n] = next_bank(Z_BANKS)
            for i in range(PACK):
                nc.tensor.transpose(z_rows[n][:, cols(i)], z_cols[n][:, cols(i)], ident[:])
            abs_z = work.tile([P, BANK], F32, name="abs_z", tag="abs_z")
            nc.scalar.activation(out=abs_z[:], in_=z_rows[n][:], func=ACT.Abs)
            if gk == 0:
                squares[j] = work.tile([P, K], F32, name="squares", tag="squares", bufs=4)
            nc.vector.tensor_tensor(out=squares[j][:, cols(gk, PASS)], in0=z_rows[n][:], in1=abs_z[:], op=ALU.mult)

        def sum_cubes(n):
            j, gk = n // PASSES, n % PASSES
            cubes = work.tile([P, BANK], F32, name="cubes", tag="cubes", bufs=2)
            cube_sums[n] = kept("cube_sum%d" % n, [P, 1], F32)
            nc.vector.scalar_tensor_tensor(
                out=cubes[:], in0=z_rows[n][:], scalar=1.0 / K, in1=squares[j][:, cols(gk, PASS)],
                op0=ALU.mult, op1=ALU.mult, accum_out=cube_sums[n][:],
            )

        def norm(j):
            mean = kept("mean%d" % j, [P, 1], F32)
            (nc.gpsimd if j < TILES - TAIL_TILES else nc.vector).tensor_scalar(
                out=mean[:], in0=cube_sums[2 * j][:], scalar1=cube_sums[2 * j + 1][:], scalar2=eps[:], op0=ALU.add, op1=ALU.add
            )
            inv_norms[j] = kept("inv_norm%d" % j, [P, 1], F32)
            nc.gpsimd.tensor_tensor(out=inv_norms[j][:], in0=mean[:], in1=exponent[:], op=ALU.pow)

        def scale_and_store(j):
            rows = out[cols(j // 2, 2 * P), :].rearrange("(p j) k -> p j k", j=2)[:, j % 2, :]
            res = work.tile([P, K], F32, name="res", tag="res", bufs=4)
            if j < TILES - TAIL_TILES:
                nc.gpsimd.tensor_scalar(out=res[:], in0=squares[j][:], scalar1=inv_norms[j][:], scalar2=0.0, op0=ALU.mult, op1=ALU.add)
                nc.sync.dma_start(out=rows, in_=res[:])
            else:
                split = K if j < TILES - 1 else LAST_SPLIT
                nc.scalar.activation(out=res[:, :split], in_=squares[j][:, :split], func=ACT.Copy, scale=inv_norms[j][:])
                nc.sync.dma_start(out=rows[:, :split], in_=res[:, :split])
                if split < K:
                    nc.vector.tensor_scalar(out=res[:, split:], in0=squares[j][:, split:], scalar1=inv_norms[j][:], scalar2=None, op0=ALU.mult)
                    nc.sync.dma_start(out=rows[:, split:], in_=res[:, split:])

        turn_a(0, warm_count=2); scale_x(0)
        turn_a(1); scale_x(1); quantize_a_k(0); quantize_a_k(1)
        turn_x(0, warm_count=2); scale_x(2)
        group_a(0, 0); quantize_x(0); scale_x(3)
        turn_a(2)
        turn_a(3); quantize_a_k(2)
        turn_x(1); quantize_a_k(3); scale_x(4)
        group_a(0, 1); quantize_x(1); widen_d()
        first_product(0); quantize_a_m(0, 0)
        turn_a(4)
        first_product(2); quantize_a_k(4); scale_x(5)
        turn_a(5)
        group_a(1, 0); quantize_a_k(5)
        turn_a(6); scale_x(6)
        turn_a(7); quantize_a_k(6)
        group_a(1, 1); quantize_a_k(7); scale_x(7)
        turn_x(2); quantize_a_m(1, 0)
        group_a(0, 2); quantize_x(2)
        turn_x(3, on_vector=True)
        first_product(1); quantize_x(3)
        group_a(0, 3, on_vector=True); quantize_u(0)
        group_a(1, 2); quantize_a_m(0, 1)
        first_product(3)
        group_a(1, 3); quantize_u(1); quantize_a_m(1, 1)

        for step in range(UNITS + BACK_LAG + 1):
            ahead, back = step + LEAD, step - BACK_LAG
            late_tile = HEAD_TILES + step // 2
            if 0 <= back < UNITS:
                signed_square(back)
            if ahead < UNITS:
                first_product(ahead)
            if step % 2 == 1 and late_tile < TILES:
                quantize_x(late_tile)
            cubed = back if ahead < UNITS else back - 1
            if cubed >= 0 and ahead != UNITS:
                sum_cubes(cubed)
                if cubed % 2 == 1:
                    norm(cubed // 2)
                    if cubed // 2 < TILES - TAIL_TILES:
                        scale_and_store(cubed // 2)
            if ahead % 2 == 1 and ahead < UNITS:
                quantize_u(ahead // 2)
            if step < UNITS:
                second_product(step)
            if step % 2 == 0 and late_tile < TILES:
                turn_x(late_tile, Z_BANKS)
        for j in range(TILES - TAIL_TILES, TILES):
            scale_and_store(j)
